import numpy as np
import ml_dtypes


def mxq(x, axis, fmt="e4m3"):
    dtype, down = {"e4m3": (ml_dtypes.float8_e4m3fn, 7), "e5m2": (ml_dtypes.float8_e5m2, 14)}[fmt]
    v = np.moveaxis(np.asarray(x, np.float32).astype(ml_dtypes.bfloat16).astype(np.float64), axis, -1)
    blocks = v.reshape(v.shape[:-1] + (-1, 32))
    amax = np.abs(blocks).max(-1, keepdims=True)
    byte = np.maximum(np.where(amax > 0, np.frexp(amax)[1] - 1 + 127, 0) - down, 1)
    scale = np.exp2(byte - 127.0)
    codes = (blocks / scale).astype(np.float32).astype(dtype).astype(np.float64)
    return np.moveaxis((codes * scale).reshape(v.shape), -1, axis)


WIDE = False


def mx_kscale(k):
    if not WIDE:
        return np.ones(k)
    levels = np.array([10, -10, 5, -5, 0])
    if k % 512:
        return np.exp2(np.random.permutation(np.resize(levels, k // 32))).repeat(32)
    a = np.empty((k // 512, 16))
    for p in range(k // 512):
        a[p, :8] = np.random.permutation(np.resize(levels, 8))
        for g in range(8):
            far = levels[np.abs(levels - a[p, g]) >= 10]
            a[p, g + 8] = far[np.random.randint(len(far))]
    return np.exp2(a.ravel()).repeat(32)


def f64(x):
    return np.asarray(x).astype(np.float64)


def striped(idx):
    return np.tile(np.asarray(idx).reshape(-1, 16).T, (8, 1)).astype(np.uint16)


def unstriped(offs):
    return offs[:16].T.reshape(-1).astype(np.int64)


E2M1 = np.array([0.0, 0.5, 1.0, 1.5, 2.0, 3.0, 4.0, 6.0, -0.0, -0.5, -1.0, -1.5, -2.0, -3.0, -4.0, -6.0])


def pack_weight(w, fmt):
    k, n = w.shape
    w = f64(np.asarray(w, np.float32).astype(ml_dtypes.bfloat16)).reshape(k // 32, 32, n)
    amax = np.abs(w).max(1)
    if fmt == "e4m3":
        byte = np.frexp(amax)[1] - 1 + 127 - 7
    else:
        mant, ex = np.frexp(amax / 6.0)
        byte = np.where(mant > 0.5, ex, ex - 1) + 127
    byte = np.clip(np.where(amax > 0, byte, 1), 1, 254)
    scaled = (w * np.exp2(127.0 - byte)[:, None, :]).reshape(k, n).astype(np.float32)
    by_word = np.ascontiguousarray(scaled.reshape(k // 512, 128, 4, n).transpose(0, 1, 3, 2))
    if fmt == "e4m3":
        words = by_word.astype(ml_dtypes.float8_e4m3fn).view(np.uint8)
    else:
        c = by_word.astype(ml_dtypes.float4_e2m1fn).view(np.uint8) & 0xF
        words = (c[..., 0::2] | (c[..., 1::2] << 4)).reshape(k // 512, 128, 2 * n)
    return np.ascontiguousarray(words), np.ascontiguousarray(byte.astype(np.uint8).reshape(k // 512, 16, n))


def unpack_weight(words, scales, fmt):
    g, _, n = scales.shape
    words = np.ascontiguousarray(words).reshape(g, 128, n, -1)
    if fmt == "e4m3":
        vals = words.view(ml_dtypes.float8_e4m3fn).astype(np.float64)
    else:
        nib = np.empty((g, 128, n, 4), np.uint8)
        nib[..., 0::2] = words & 0xF
        nib[..., 1::2] = words >> 4
        vals = E2M1[nib]
    vals = vals * np.repeat(np.exp2(scales.astype(np.float64) - 127.0), 8, axis=1)[..., None]
    return vals.transpose(0, 1, 3, 2).reshape(g * 512, n)


K, T, I, F, M = 512, 2048, 512, 512, 128


def setup_inputs():
    n = np.random.standard_normal
    idx = np.random.permutation(T)[:I]
    fk = mx_kscale(K)
    ff = mx_kscale(F)
    encp = pack_weight(n((K, T)) / fk[:, None], "e4m3")
    return {
        "enc_words": encp[0],
        "enc_scales": encp[1],
        "wk": (n((K, F)) * 1 / np.sqrt(K) * fk[:, None]).astype(np.float32),
        "qterm": (0.5 * n((F, 1))).astype(np.float32),
        "gain": (np.random.uniform(0.5, 2.0, (F, 1)) * ff[:, None]).astype(np.float32),
        "score": (n((F, M)) * 0.8 / np.sqrt(F) / ff[:, None]).astype(np.float32),
        "offs": striped(idx),
    }


def reference(enc_words, enc_scales, wk, qterm, gain, score, offs):
    idx = unstriped(offs)
    encu = unpack_weight(enc_words, enc_scales, "e4m3")
    wkq = mxq(f64(wk), 0, "e4m3")
    encidxg = encu[:, idx]
    z = wkq.T @ encidxg
    h1 = np.tanh(z + f64(qterm)) * f64(gain)
    scoreq = mxq(f64(score), 0, "e4m3")
    h1q = mxq(h1, 0, "e4m3")
    a = scoreq.T @ h1q
    p = np.exp(a - np.max(a, axis=1, keepdims=True))
    y = p / np.sum(p, axis=1, keepdims=True) * 512.0
    return y

@@ -1,0 +1,143 @@
+from contextlib import ExitStack
+
+import concourse.mybir as mybir
+
+K, T, I, F, M = 512, 2048, 512, 512, 128
+FLOPS = 2 * K * F * I + 2 * F * M * I
+
+F32 = mybir.dt.float32
+BF16 = mybir.dt.bfloat16
+I32 = mybir.dt.int32
+U32 = mybir.dt.uint32
+U16 = mybir.dt.uint16
+U8 = mybir.dt.uint8
+FP8X4 = mybir.dt.float8_e4m3fn_x4
+ACT = mybir.ActivationFunctionType
+ALU = mybir.AluOpType
+AXIS = mybir.AxisListType
+
+P = 128
+PACK = 4
+CHUNK = 128
+GATHER = 256
+WK_VECTOR_COLS = 80
+PIECES = (64, 64, 128, 128, 128)
+
+
+def tile_attend_additiveattn_kernel(tc, enc_words, enc_scales, wk, qterm, gain, score, offs, out):
+    nc = tc.nc
+    with ExitStack() as ctx:
+        keep = ctx.enter_context(tc.tile_pool(name="keep", bufs=1))
+        zpool = ctx.enter_context(tc.psum_pool(name="zpool", bufs=7))
+        apool = ctx.enter_context(tc.psum_pool(name="apool", bufs=1))
+
+        offsets = keep.tile([P, I // 16], U16, name="offsets")
+        nc.sync.dma_start(offsets[:], offs)
+        pool_scales = keep.tile([P, T], U8, name="pool_scales", align_bytes=64)
+        nc.vector.memset(pool_scales[:].bitcast(I32), 0)
+        wk_raw = keep.tile([P, PACK, F], F32, name="wk_raw")
+        wk_rows = wk.rearrange("(p j) f -> p j f", j=PACK)
+        nc.sync.dma_start(wk_raw[:, :2], wk_rows[:, :2])
+        for quad in range(4):
+            nc.sync.dma_start(
+                pool_scales[32 * quad : 32 * quad + 4, :].bitcast(I32),
+                enc_scales[0, 4 * quad : 4 * quad + 4, :].bitcast(I32),
+            )
+        nc.sync.dma_start(wk_raw[:, 2:], wk_rows[:, 2:])
+        pool_words = keep.tile([P, T], I32, name="pool_words", align_bytes=64)
+        nc.sync.dma_start(pool_words[:], enc_words[0].rearrange("p n r -> p (n r)").bitcast(I32))
+        q_cols = keep.tile([P, PACK], F32, name="q_cols")
+        nc.sync.dma_start(q_cols[:], qterm.rearrange("(p t) o -> p (t o)", t=PACK))
+        gain_cols = keep.tile([P, PACK], F32, name="gain_cols")
+        nc.sync.dma_start(gain_cols[:], gain.rearrange("(p t) o -> p (t o)", t=PACK))
+        score_raw = keep.tile([P, PACK, M], F32, name="score_raw")
+        nc.sync.dma_start(score_raw[:], score.rearrange("(p j) m -> p j m", j=PACK))
+
+        enc_sc = keep.tile([P, I], U8, name="enc_sc", align_bytes=64)
+        nc.vector.tensor_copy(enc_sc[:], pool_scales[:].indirect(offsets[:]))
+
+        wk_bf = keep.tile([P, PACK, P, PACK], BF16, name="wk_bf", align_bytes=64)
+        src = wk_raw[:].rearrange("p j (m t) -> p m j t", t=PACK)
+        dst = wk_bf[:].rearrange("p t m j -> p m j t")
+        nc.vector.tensor_copy(dst[:, :WK_VECTOR_COLS], src[:, :WK_VECTOR_COLS])
+        nc.scalar.activation(dst[:, WK_VECTOR_COLS:], src[:, WK_VECTOR_COLS:], ACT.Copy)
+        wk_codes = keep.tile([P, F], U32, name="wk_codes", tag="wk_codes_then_score", align_bytes=64)
+        wk_sc = keep.tile([P, F], U8, name="wk_sc", align_bytes=64)
+        nc.vector.quantize_mx(
+            wk_codes[:].bitcast(FP8X4), wk_sc[:], wk_bf[:].rearrange("p t m j -> p (t m j)")
+        )
+
+        enc_codes = []
+        for g in range(I // GATHER):
+            picked = keep.tile([P, GATHER], U32, name=f"enc_codes{g}", align_bytes=64)
+            nc.vector.tensor_copy(
+                picked[:],
+                pool_words[:].bitcast(U32).indirect(offsets[:, g * GATHER // 16 : (g + 1) * GATHER // 16]),
+            )
+            enc_codes.append(picked)
+
+        starts = [sum(PIECES[:n]) for n in range(len(PIECES))]
+        th = [keep.tile([P, PACK, w], F32, name=f"th{n}") for n, w in enumerate(PIECES)]
+        chunks = I // CHUNK
+        h_bf = [keep.tile([P, CHUNK, PACK], BF16, name=f"h_bf{c}", align_bytes=64) for c in range(chunks)]
+        h_codes = [keep.tile([P, CHUNK], U32, name=f"h_codes{c}", align_bytes=64) for c in range(chunks)]
+        h_sc = [keep.tile([P, CHUNK], U8, name=f"h_sc{c}", align_bytes=64) for c in range(chunks)]
+        logits = apool.tile([P, I], F32, name="logits")
+
+        for n, (i0, w) in enumerate(zip(starts, PIECES)):
+            picked = enc_codes[i0 // GATHER][:, i0 % GATHER : i0 % GATHER + w]
+            for t in range(PACK):
+                rows = slice(t * P, (t + 1) * P)
+                z = zpool.tile([P, w], F32, name="z")
+                nc.tensor.matmul_mx(
+                    z[:], lhsT=wk_codes[:, rows].bitcast(FP8X4), lhsT_scale=wk_sc[:, rows],
+                    rhs=picked.bitcast(FP8X4), rhs_scale=enc_sc[:, i0 : i0 + w], start=True, stop=True,
+                )
+                nc.scalar.activation(th[n][:, t, :], z[:], ACT.Tanh, bias=q_cols[:, t : t + 1])
+
+        score_bf = keep.tile([P, M, PACK], BF16, name="score_bf", tag="wk_codes_then_score", align_bytes=64)
+        nc.scalar.activation(
+            score_bf[:].rearrange("p (a b) j -> p a j b", b=4),
+            score_raw[:].rearrange("p j (a b) -> p a j b", b=4),
+            ACT.Copy,
+        )
+        score_codes = keep.tile([P, M], U32, name="score_codes", align_bytes=64)
+        score_sc = keep.tile([P, M], U8, name="score_sc", align_bytes=64)
+
+        def apply_gain(n):
+            i0, w = starts[n], PIECES[n]
+            nc.vector.tensor_tensor(
+                h_bf[i0 // CHUNK][:, i0 % CHUNK : i0 % CHUNK + w].rearrange("p (a b) t -> p a t b", b=4),
+                th[n][:].rearrange("p t (a b) -> p a t b", b=4),
+                gain_cols[:].rearrange("p (a t b) -> p a t b", a=1, b=1).to_broadcast([P, w // 4, PACK, 4]),
+                ALU.mult,
+            )
+
+        def quantize_h(c):
+            nc.vector.quantize_mx(h_codes[c][:].bitcast(FP8X4), h_sc[c][:], h_bf[c][:].rearrange("p i t -> p (i t)"))
+
+        apply_gain(0)
+        apply_gain(1)
+        for c in range(1, chunks):
+            apply_gain(c + 1)
+            quantize_h(c - 1)
+        nc.vector.quantize_mx(score_codes[:].bitcast(FP8X4), score_sc[:], score_bf[:].rearrange("p m j -> p (m j)"))
+        quantize_h(chunks - 1)
+        for c in range(chunks):
+            nc.tensor.matmul_mx(
+                logits[:, c * CHUNK : (c + 1) * CHUNK], lhsT=score_codes[:].bitcast(FP8X4), lhsT_scale=score_sc[:],
+                rhs=h_codes[c][:].bitcast(FP8X4), rhs_scale=h_sc[c][:], start=True, stop=True,
+            )
+
+        neg_max = keep.tile([P, 1], F32, name="neg_max")
+        nc.vector.tensor_reduce(neg_max[:], logits[:], AXIS.X, ALU.max, negate=True)
+        p_exp = keep.tile([P, I], F32, name="p_exp")
+        row_sum = keep.tile([P, 1], F32, name="row_sum")
+        nc.scalar.activation(p_exp[:], logits[:], ACT.Exp, bias=neg_max[:], accum_out=row_sum[:])
+        inv_sum = keep.tile([P, 1], F32, name="inv_sum")
+        nc.vector.reciprocal(inv_sum[:], row_sum[:])
+        result = keep.tile([P, I], F32, name="result")
+        for half, queue in enumerate((nc.sync, nc.scalar)):
+            cols = slice(half * I // 2, (half + 1) * I // 2)
+            nc.vector.tensor_scalar(result[:, cols], p_exp[:, cols], inv_sum[:], 512.0, ALU.mult, ALU.mult)
+            queue.dma_start(out[:, cols], result[:, cols])

@@ -21,47 +21,49 @@ PACK = 4
 CHUNK = 128
 GATHER = 256
 WK_VECTOR_COLS = 80
-PIECES = (64, 64, 128, 128, 128)
+PIECES = (128, 128, 128, 128)
 
 
 def tile_attend_additiveattn_kernel(tc, enc_words, enc_scales, wk, qterm, gain, score, offs, out):
     nc = tc.nc
     with ExitStack() as ctx:
         keep = ctx.enter_context(tc.tile_pool(name="keep", bufs=1))
-        zpool = ctx.enter_context(tc.psum_pool(name="zpool", bufs=7))
+        zpool = ctx.enter_context(tc.psum_pool(name="zpool", bufs=6))
         apool = ctx.enter_context(tc.psum_pool(name="apool", bufs=1))
+
+        warm = keep.tile([P, 1], F32, name="warm")
+        nc.gpsimd.memset(warm[:], 0.0)
+        warm_out = keep.tile([P, 1], F32, name="warm_out")
+        nc.scalar.activation(warm_out[:], warm[:], ACT.Exp)
 
         offsets = keep.tile([P, I // 16], U16, name="offsets")
         nc.sync.dma_start(offsets[:], offs)
         pool_scales = keep.tile([P, T], U8, name="pool_scales", align_bytes=64)
         nc.vector.memset(pool_scales[:].bitcast(I32), 0)
-        wk_raw = keep.tile([P, PACK, F], F32, name="wk_raw")
+        wk_raw = keep.tile([P, PACK, F], F32, name="wk_raw", tag="shared1", align_bytes=64)
         wk_rows = wk.rearrange("(p j) f -> p j f", j=PACK)
         nc.sync.dma_start(wk_raw[:, :2], wk_rows[:, :2])
-        for quad in range(4):
-            nc.sync.dma_start(
-                pool_scales[32 * quad : 32 * quad + 4, :].bitcast(I32),
-                enc_scales[0, 4 * quad : 4 * quad + 4, :].bitcast(I32),
-            )
+        for r in range(4):
+            nc.sync.dma_start(pool_scales[r:P:32, :].bitcast(I32), enc_scales[0, r:16:4, :].bitcast(I32))
         nc.sync.dma_start(wk_raw[:, 2:], wk_rows[:, 2:])
         pool_words = keep.tile([P, T], I32, name="pool_words", align_bytes=64)
         nc.sync.dma_start(pool_words[:], enc_words[0].rearrange("p n r -> p (n r)").bitcast(I32))
         q_cols = keep.tile([P, PACK], F32, name="q_cols")
         nc.sync.dma_start(q_cols[:], qterm.rearrange("(p t) o -> p (t o)", t=PACK))
-        gain_cols = keep.tile([P, PACK], F32, name="gain_cols")
-        nc.sync.dma_start(gain_cols[:], gain.rearrange("(p t) o -> p (t o)", t=PACK))
         score_raw = keep.tile([P, PACK, M], F32, name="score_raw")
         nc.sync.dma_start(score_raw[:], score.rearrange("(p j) m -> p j m", j=PACK))
+        gain_cols = keep.tile([P, PACK], F32, name="gain_cols")
+        nc.sync.dma_start(gain_cols[:], gain.rearrange("(p t) o -> p (t o)", t=PACK))
 
         enc_sc = keep.tile([P, I], U8, name="enc_sc", align_bytes=64)
         nc.vector.tensor_copy(enc_sc[:], pool_scales[:].indirect(offsets[:]))
 
-        wk_bf = keep.tile([P, PACK, P, PACK], BF16, name="wk_bf", align_bytes=64)
+        wk_bf = keep.tile([P, PACK, P, PACK], BF16, name="wk_bf", tag="shared0", align_bytes=64)
         src = wk_raw[:].rearrange("p j (m t) -> p m j t", t=PACK)
         dst = wk_bf[:].rearrange("p t m j -> p m j t")
         nc.vector.tensor_copy(dst[:, :WK_VECTOR_COLS], src[:, :WK_VECTOR_COLS])
         nc.scalar.activation(dst[:, WK_VECTOR_COLS:], src[:, WK_VECTOR_COLS:], ACT.Copy)
-        wk_codes = keep.tile([P, F], U32, name="wk_codes", tag="wk_codes_then_score", align_bytes=64)
+        wk_codes = keep.tile([P, F], U32, name="wk_codes", align_bytes=64)
         wk_sc = keep.tile([P, F], U8, name="wk_sc", align_bytes=64)
         nc.vector.quantize_mx(
             wk_codes[:].bitcast(FP8X4), wk_sc[:], wk_bf[:].rearrange("p t m j -> p (t m j)")
@@ -69,12 +71,21 @@ def tile_attend_additiveattn_kernel(tc, enc_words, enc_scales, wk, qterm, gain, 
 
         enc_codes = []
         for g in range(I // GATHER):
-            picked = keep.tile([P, GATHER], U32, name=f"enc_codes{g}", align_bytes=64)
+            picked = keep.tile([P, GATHER], U32, name=f"enc_codes{g}", tag=f"shared{g}", align_bytes=64)
             nc.vector.tensor_copy(
                 picked[:],
                 pool_words[:].bitcast(U32).indirect(offsets[:, g * GATHER // 16 : (g + 1) * GATHER // 16]),
             )
             enc_codes.append(picked)
+
+        score_bf = keep.tile([P, M, PACK], BF16, name="score_bf", align_bytes=64)
+        nc.vector.tensor_copy(
+            score_bf[:].rearrange("p (a b) j -> p a j b", b=4),
+            score_raw[:].rearrange("p j (a b) -> p a j b", b=4),
+        )
+        score_codes = keep.tile([P, M], U32, name="score_codes", align_bytes=64)
+        score_sc = keep.tile([P, M], U8, name="score_sc", align_bytes=64)
+        nc.vector.quantize_mx(score_codes[:].bitcast(FP8X4), score_sc[:], score_bf[:].rearrange("p m j -> p (m j)"))
 
         starts = [sum(PIECES[:n]) for n in range(len(PIECES))]
         th = [keep.tile([P, PACK, w], F32, name=f"th{n}") for n, w in enumerate(PIECES)]
@@ -82,7 +93,9 @@ def tile_attend_additiveattn_kernel(tc, enc_words, enc_scales, wk, qterm, gain, 
         h_bf = [keep.tile([P, CHUNK, PACK], BF16, name=f"h_bf{c}", align_bytes=64) for c in range(chunks)]
         h_codes = [keep.tile([P, CHUNK], U32, name=f"h_codes{c}", align_bytes=64) for c in range(chunks)]
         h_sc = [keep.tile([P, CHUNK], U8, name=f"h_sc{c}", align_bytes=64) for c in range(chunks)]
-        logits = apool.tile([P, I], F32, name="logits")
+        early = I // 2
+        logits_a = apool.tile([P, early], F32, name="logits_a")
+        logits_b = apool.tile([P, I - early], F32, name="logits_b")
 
         for n, (i0, w) in enumerate(zip(starts, PIECES)):
             picked = enc_codes[i0 // GATHER][:, i0 % GATHER : i0 % GATHER + w]
@@ -94,15 +107,6 @@ def tile_attend_additiveattn_kernel(tc, enc_words, enc_scales, wk, qterm, gain, 
                     rhs=picked.bitcast(FP8X4), rhs_scale=enc_sc[:, i0 : i0 + w], start=True, stop=True,
                 )
                 nc.scalar.activation(th[n][:, t, :], z[:], ACT.Tanh, bias=q_cols[:, t : t + 1])
-
-        score_bf = keep.tile([P, M, PACK], BF16, name="score_bf", tag="wk_codes_then_score", align_bytes=64)
-        nc.scalar.activation(
-            score_bf[:].rearrange("p (a b) j -> p a j b", b=4),
-            score_raw[:].rearrange("p j (a b) -> p a j b", b=4),
-            ACT.Copy,
-        )
-        score_codes = keep.tile([P, M], U32, name="score_codes", align_bytes=64)
-        score_sc = keep.tile([P, M], U8, name="score_sc", align_bytes=64)
 
         def apply_gain(n):
             i0, w = starts[n], PIECES[n]
@@ -117,23 +121,24 @@ def tile_attend_additiveattn_kernel(tc, enc_words, enc_scales, wk, qterm, gain, 
             nc.vector.quantize_mx(h_codes[c][:].bitcast(FP8X4), h_sc[c][:], h_bf[c][:].rearrange("p i t -> p (i t)"))
 
         apply_gain(0)
-        apply_gain(1)
         for c in range(1, chunks):
-            apply_gain(c + 1)
+            apply_gain(c)
             quantize_h(c - 1)
-        nc.vector.quantize_mx(score_codes[:].bitcast(FP8X4), score_sc[:], score_bf[:].rearrange("p m j -> p (m j)"))
         quantize_h(chunks - 1)
         for c in range(chunks):
             nc.tensor.matmul_mx(
-                logits[:, c * CHUNK : (c + 1) * CHUNK], lhsT=score_codes[:].bitcast(FP8X4), lhsT_scale=score_sc[:],
+                (logits_a, logits_b)[c // 2][:, c % 2 * CHUNK : (c % 2 + 1) * CHUNK], lhsT=score_codes[:].bitcast(FP8X4), lhsT_scale=score_sc[:],
                 rhs=h_codes[c][:].bitcast(FP8X4), rhs_scale=h_sc[c][:], start=True, stop=True,
             )
 
+        neg_logits = keep.tile([P, I], F32, name="neg_logits")
+        neg_max_a = keep.tile([P, 1], F32, name="neg_max_a")
+        nc.vector.tensor_scalar(neg_logits[:, :early], logits_a[:], -1.0, None, ALU.mult, ALU.min, accum_out=neg_max_a[:])
         neg_max = keep.tile([P, 1], F32, name="neg_max")
-        nc.vector.tensor_reduce(neg_max[:], logits[:], AXIS.X, ALU.max, negate=True)
+        nc.vector.tensor_scalar(neg_logits[:, early:], logits_b[:], -1.0, neg_max_a[:], ALU.mult, ALU.min, accum_out=neg_max[:])
         p_exp = keep.tile([P, I], F32, name="p_exp")
         row_sum = keep.tile([P, 1], F32, name="row_sum")
-        nc.scalar.activation(p_exp[:], logits[:], ACT.Exp, bias=neg_max[:], accum_out=row_sum[:])
+        nc.scalar.activation(p_exp[:], neg_logits[:], ACT.Exp, bias=neg_max[:], scale=-1.0, accum_out=row_sum[:])
         inv_sum = keep.tile([P, 1], F32, name="inv_sum")
         nc.vector.reciprocal(inv_sum[:], row_sum[:])
         result = keep.tile([P, I], F32, name="result")

@@ -21,6 +21,7 @@ PACK = 4
 CHUNK = 128
 GATHER = 256
 WK_VECTOR_COLS = 80
+WK_FIRST = 768
 PIECES = (128, 128, 128, 128)
 
 
@@ -31,32 +32,38 @@ def tile_attend_additiveattn_kernel(tc, enc_words, enc_scales, wk, qterm, gain, 
         zpool = ctx.enter_context(tc.psum_pool(name="zpool", bufs=6))
         apool = ctx.enter_context(tc.psum_pool(name="apool", bufs=1))
 
+        offsets = keep.tile([P, I // 16], U16, name="offsets")
+        nc.sync.dma_start(offsets[:], offs)
+        pool_scales = keep.tile([P, T], U8, name="pool_scales", tag="shared2", align_bytes=64)
+        nc.vector.memset(pool_scales[:, : T // 2].bitcast(I32), 0)
+        nc.gpsimd.memset(pool_scales[:, T // 2 :].bitcast(I32), 0)
+        wk_raw = keep.tile([P, PACK, F], F32, name="wk_raw", tag="shared1", align_bytes=64)
+        wk_rows = wk.rearrange("(p j) f -> p (j f)", j=PACK)
+        wk_flat = wk_raw[:].rearrange("p j f -> p (j f)")
+        nc.sync.dma_start(wk_flat[:, :WK_FIRST], wk_rows[:, :WK_FIRST])
+        nc.sync.dma_start(pool_scales[0:P:8, :].bitcast(I32), enc_scales[0].bitcast(I32))
+        nc.sync.dma_start(wk_flat[:, WK_FIRST:], wk_rows[:, WK_FIRST:])
         warm = keep.tile([P, 1], F32, name="warm")
-        nc.gpsimd.memset(warm[:], 0.0)
+        nc.vector.memset(warm[:], 0.0)
         warm_out = keep.tile([P, 1], F32, name="warm_out")
         nc.scalar.activation(warm_out[:], warm[:], ACT.Exp)
 
-        offsets = keep.tile([P, I // 16], U16, name="offsets")
-        nc.sync.dma_start(offsets[:], offs)
-        pool_scales = keep.tile([P, T], U8, name="pool_scales", align_bytes=64)
-        nc.vector.memset(pool_scales[:].bitcast(I32), 0)
-        wk_raw = keep.tile([P, PACK, F], F32, name="wk_raw", tag="shared1", align_bytes=64)
-        wk_rows = wk.rearrange("(p j) f -> p j f", j=PACK)
-        nc.sync.dma_start(wk_raw[:, :2], wk_rows[:, :2])
-        for r in range(4):
-            nc.sync.dma_start(pool_scales[r:P:32, :].bitcast(I32), enc_scales[0, r:16:4, :].bitcast(I32))
-        nc.sync.dma_start(wk_raw[:, 2:], wk_rows[:, 2:])
         pool_words = keep.tile([P, T], I32, name="pool_words", align_bytes=64)
         nc.sync.dma_start(pool_words[:], enc_words[0].rearrange("p n r -> p (n r)").bitcast(I32))
-        q_cols = keep.tile([P, PACK], F32, name="q_cols")
-        nc.sync.dma_start(q_cols[:], qterm.rearrange("(p t) o -> p (t o)", t=PACK))
-        score_raw = keep.tile([P, PACK, M], F32, name="score_raw")
-        nc.sync.dma_start(score_raw[:], score.rearrange("(p j) m -> p j m", j=PACK))
-        gain_cols = keep.tile([P, PACK], F32, name="gain_cols")
-        nc.sync.dma_start(gain_cols[:], gain.rearrange("(p t) o -> p (t o)", t=PACK))
-
+        picked_sc = keep.tile([P, I], U8, name="picked_sc", align_bytes=64)
+        nc.vector.tensor_copy(picked_sc[:], pool_scales[:].indirect(offsets[:]))
         enc_sc = keep.tile([P, I], U8, name="enc_sc", align_bytes=64)
-        nc.vector.tensor_copy(enc_sc[:], pool_scales[:].indirect(offsets[:]))
+        nc.gpsimd.memset(enc_sc[:].bitcast(I32), 0)
+        for r in range(4):
+            nc.sync.dma_start(enc_sc[r:P:32, :].bitcast(I32), picked_sc[8 * r : P : 32, :].bitcast(I32))
+        late = keep.tile([P, PACK * M + 16], F32, name="late", tag="shared2", align_bytes=64)
+        q_cols = late[:, PACK * M : PACK * M + PACK]
+        nc.sync.dma_start(q_cols, qterm.rearrange("(p t) o -> p (t o)", t=PACK))
+        score_raw = late[:, : PACK * M].rearrange("p (j m) -> p j m", j=PACK)
+        nc.sync.dma_start(score_raw, score.rearrange("(p j) m -> p j m", j=PACK))
+        gain_cols = late[:, PACK * M + 8 : PACK * M + 8 + PACK]
+        nc.sync.dma_start(gain_cols, gain.rearrange("(p t) o -> p (t o)", t=PACK))
+
 
         wk_bf = keep.tile([P, PACK, P, PACK], BF16, name="wk_bf", tag="shared0", align_bytes=64)
         src = wk_raw[:].rearrange("p j (m t) -> p m j t", t=PACK)
@@ -71,7 +78,7 @@ def tile_attend_additiveattn_kernel(tc, enc_words, enc_scales, wk, qterm, gain, 
 
         enc_codes = []
         for g in range(I // GATHER):
-            picked = keep.tile([P, GATHER], U32, name=f"enc_codes{g}", tag=f"shared{g}", align_bytes=64)
+            picked = keep.tile([P, GATHER], U32, name=f"enc_codes{g}", tag=f"shared{1 - g}", align_bytes=64)
             nc.vector.tensor_copy(
                 picked[:],
                 pool_words[:].bitcast(U32).indirect(offsets[:, g * GATHER // 16 : (g + 1) * GATHER // 16]),
@@ -81,7 +88,7 @@ def tile_attend_additiveattn_kernel(tc, enc_words, enc_scales, wk, qterm, gain, 
         score_bf = keep.tile([P, M, PACK], BF16, name="score_bf", align_bytes=64)
         nc.vector.tensor_copy(
             score_bf[:].rearrange("p (a b) j -> p a j b", b=4),
-            score_raw[:].rearrange("p j (a b) -> p a j b", b=4),
+            score_raw.rearrange("p j (a b) -> p a j b", b=4),
         )
         score_codes = keep.tile([P, M], U32, name="score_codes", align_bytes=64)
         score_sc = keep.tile([P, M], U8, name="score_sc", align_bytes=64)
@@ -90,7 +97,7 @@ def tile_attend_additiveattn_kernel(tc, enc_words, enc_scales, wk, qterm, gain, 
         starts = [sum(PIECES[:n]) for n in range(len(PIECES))]
         th = [keep.tile([P, PACK, w], F32, name=f"th{n}") for n, w in enumerate(PIECES)]
         chunks = I // CHUNK
-        h_bf = [keep.tile([P, CHUNK, PACK], BF16, name=f"h_bf{c}", align_bytes=64) for c in range(chunks)]
+        h_bf = [keep.tile([P, CHUNK, PACK], BF16, name=f"h_bf{c}", tag=f"h_bf{c}", align_bytes=64) for c in range(chunks)]
         h_codes = [keep.tile([P, CHUNK], U32, name=f"h_codes{c}", align_bytes=64) for c in range(chunks)]
         h_sc = [keep.tile([P, CHUNK], U8, name=f"h_sc{c}", align_bytes=64) for c in range(chunks)]
         early = I // 2
@@ -113,7 +120,7 @@ def tile_attend_additiveattn_kernel(tc, enc_words, enc_scales, wk, qterm, gain, 
             nc.vector.tensor_tensor(
                 h_bf[i0 // CHUNK][:, i0 % CHUNK : i0 % CHUNK + w].rearrange("p (a b) t -> p a t b", b=4),
                 th[n][:].rearrange("p t (a b) -> p a t b", b=4),
-                gain_cols[:].rearrange("p (a t b) -> p a t b", a=1, b=1).to_broadcast([P, w // 4, PACK, 4]),
+                gain_cols.rearrange("p (a t b) -> p a t b", a=1, b=1).to_broadcast([P, w // 4, PACK, 4]),
                 ALU.mult,
             )
 
@@ -131,7 +138,7 @@ def tile_attend_additiveattn_kernel(tc, enc_words, enc_scales, wk, qterm, gain, 
                 rhs=h_codes[c][:].bitcast(FP8X4), rhs_scale=h_sc[c][:], start=True, stop=True,
             )
 
-        neg_logits = keep.tile([P, I], F32, name="neg_logits")
+        neg_logits = keep.tile([P, I], F32, name="neg_logits", tag=f"h_bf{chunks - 2}", align_bytes=64)
         neg_max_a = keep.tile([P, 1], F32, name="neg_max_a")
         nc.vector.tensor_scalar(neg_logits[:, :early], logits_a[:], -1.0, None, ALU.mult, ALU.min, accum_out=neg_max_a[:])
         neg_max = keep.tile([P, 1], F32, name="neg_max")

@@ -149,7 +149,5 @@ def tile_attend_additiveattn_kernel(tc, enc_words, enc_scales, wk, qterm, gain, 
         inv_sum = keep.tile([P, 1], F32, name="inv_sum")
         nc.vector.reciprocal(inv_sum[:], row_sum[:])
         result = keep.tile([P, I], F32, name="result")
-        for half, queue in enumerate((nc.sync, nc.scalar)):
-            cols = slice(half * I // 2, (half + 1) * I // 2)
-            nc.vector.tensor_scalar(result[:, cols], p_exp[:, cols], inv_sum[:], 512.0, ALU.mult, ALU.mult)
-            queue.dma_start(out[:, cols], result[:, cols])
+        nc.vector.tensor_scalar(result[:], p_exp[:], inv_sum[:], 512.0, ALU.mult, ALU.mult)
+        nc.sync.dma_start(out, result[:])

@@ -22,6 +22,7 @@ CHUNK = 128
 GATHER = 256
 WK_VECTOR_COLS = 80
 WK_FIRST = 768
+LAST_SCALAR_SLOTS = 32
 PIECES = (128, 128, 128, 128)
 
 
@@ -33,7 +34,6 @@ def tile_attend_additiveattn_kernel(tc, enc_words, enc_scales, wk, qterm, gain, 
         apool = ctx.enter_context(tc.psum_pool(name="apool", bufs=1))
 
         offsets = keep.tile([P, I // 16], U16, name="offsets")
-        nc.sync.dma_start(offsets[:], offs)
         pool_scales = keep.tile([P, T], U8, name="pool_scales", tag="shared2", align_bytes=64)
         nc.vector.memset(pool_scales[:, : T // 2].bitcast(I32), 0)
         nc.gpsimd.memset(pool_scales[:, T // 2 :].bitcast(I32), 0)
@@ -41,7 +41,8 @@ def tile_attend_additiveattn_kernel(tc, enc_words, enc_scales, wk, qterm, gain, 
         wk_rows = wk.rearrange("(p j) f -> p (j f)", j=PACK)
         wk_flat = wk_raw[:].rearrange("p j f -> p (j f)")
         nc.sync.dma_start(wk_flat[:, :WK_FIRST], wk_rows[:, :WK_FIRST])
-        nc.sync.dma_start(pool_scales[0:P:8, :].bitcast(I32), enc_scales[0].bitcast(I32))
+        nc.sync.dma_start(offsets[:], offs)
+        nc.sync.dma_start(pool_scales[32:96:4, :].bitcast(I32), enc_scales[0].bitcast(I32))
         nc.sync.dma_start(wk_flat[:, WK_FIRST:], wk_rows[:, WK_FIRST:])
         warm = keep.tile([P, 1], F32, name="warm")
         nc.vector.memset(warm[:], 0.0)
@@ -55,7 +56,7 @@ def tile_attend_additiveattn_kernel(tc, enc_words, enc_scales, wk, qterm, gain, 
         enc_sc = keep.tile([P, I], U8, name="enc_sc", align_bytes=64)
         nc.gpsimd.memset(enc_sc[:].bitcast(I32), 0)
         for r in range(4):
-            nc.sync.dma_start(enc_sc[r:P:32, :].bitcast(I32), picked_sc[8 * r : P : 32, :].bitcast(I32))
+            nc.sync.dma_start(enc_sc[r:P:32, :].bitcast(I32), picked_sc[32 + 4 * r : 96 : 16, :].bitcast(I32))
         late = keep.tile([P, PACK * M + 16], F32, name="late", tag="shared2", align_bytes=64)
         q_cols = late[:, PACK * M : PACK * M + PACK]
         nc.sync.dma_start(q_cols, qterm.rearrange("(p t) o -> p (t o)", t=PACK))
@@ -117,9 +118,13 @@ def tile_attend_additiveattn_kernel(tc, enc_words, enc_scales, wk, qterm, gain, 
 
         def apply_gain(n):
             i0, w = starts[n], PIECES[n]
+            if n == len(PIECES) - 1:
+                w = w - LAST_SCALAR_SLOTS
+                for t in range(PACK):
+                    nc.scalar.activation(h_bf[n][:, w:, t], th[n][:, t, w:], ACT.Copy, scale=gain_cols[:, t : t + 1])
             nc.vector.tensor_tensor(
                 h_bf[i0 // CHUNK][:, i0 % CHUNK : i0 % CHUNK + w].rearrange("p (a b) t -> p a t b", b=4),
-                th[n][:].rearrange("p t (a b) -> p a t b", b=4),
+                th[n][:, :, :w].rearrange("p t (a b) -> p a t b", b=4),
                 gain_cols.rearrange("p (a t b) -> p a t b", a=1, b=1).to_broadcast([P, w // 4, PACK, 4]),
                 ALU.mult,
             )

@@ -42,7 +42,7 @@ def tile_attend_additiveattn_kernel(tc, enc_words, enc_scales, wk, qterm, gain, 
         wk_flat = wk_raw[:].rearrange("p j f -> p (j f)")
         nc.sync.dma_start(wk_flat[:, :WK_FIRST], wk_rows[:, :WK_FIRST])
         nc.sync.dma_start(offsets[:], offs)
-        nc.sync.dma_start(pool_scales[32:96:4, :].bitcast(I32), enc_scales[0].bitcast(I32))
+        nc.sync.dma_start(pool_scales[0:P:8, :].bitcast(I32), enc_scales[0].bitcast(I32))
         nc.sync.dma_start(wk_flat[:, WK_FIRST:], wk_rows[:, WK_FIRST:])
         warm = keep.tile([P, 1], F32, name="warm")
         nc.vector.memset(warm[:], 0.0)
@@ -54,9 +54,9 @@ def tile_attend_additiveattn_kernel(tc, enc_words, enc_scales, wk, qterm, gain, 
         picked_sc = keep.tile([P, I], U8, name="picked_sc", align_bytes=64)
         nc.vector.tensor_copy(picked_sc[:], pool_scales[:].indirect(offsets[:]))
         enc_sc = keep.tile([P, I], U8, name="enc_sc", align_bytes=64)
-        nc.gpsimd.memset(enc_sc[:].bitcast(I32), 0)
-        for r in range(4):
-            nc.sync.dma_start(enc_sc[r:P:32, :].bitcast(I32), picked_sc[32 + 4 * r : 96 : 16, :].bitcast(I32))
+        nc.vector.tensor_copy(enc_sc[:].bitcast(I32), picked_sc[:].bitcast(I32))
+        for r in range(1, 4):
+            nc.sync.dma_start(enc_sc[r:P:32, :].bitcast(I32), picked_sc[8 * r : P : 32, :].bitcast(I32))
         late = keep.tile([P, PACK * M + 16], F32, name="late", tag="shared2", align_bytes=64)
         q_cols = late[:, PACK * M : PACK * M + PACK]
         nc.sync.dma_start(q_cols, qterm.rearrange("(p t) o -> p (t o)", t=PACK))

@@ -14,36 +14,43 @@ U8 = mybir.dt.uint8
 FP8X4 = mybir.dt.float8_e4m3fn_x4
 ACT = mybir.ActivationFunctionType
 ALU = mybir.AluOpType
-AXIS = mybir.AxisListType
 
 P = 128
 PACK = 4
+QUADRANT = 32
+ROW_STEP = 8
+RUN = 4
 CHUNK = 128
+CHUNKS = I // CHUNK
 GATHER = 256
-WK_VECTOR_COLS = 80
+Z_BANKS = 6
 WK_FIRST = 768
+WK_VECTOR_COLS = 80
 LAST_SCALAR_SLOTS = 32
-PIECES = (128, 128, 128, 128)
+AFTER_WK_QUANTISER = "shared0"
+AFTER_WK_CAST = "shared1"
+AFTER_SCALE_GATHER = "shared2"
 
 
 def tile_attend_additiveattn_kernel(tc, enc_words, enc_scales, wk, qterm, gain, score, offs, out):
     nc = tc.nc
     with ExitStack() as ctx:
         keep = ctx.enter_context(tc.tile_pool(name="keep", bufs=1))
-        zpool = ctx.enter_context(tc.psum_pool(name="zpool", bufs=6))
+        zpool = ctx.enter_context(tc.psum_pool(name="zpool", bufs=Z_BANKS))
         apool = ctx.enter_context(tc.psum_pool(name="apool", bufs=1))
 
         offsets = keep.tile([P, I // 16], U16, name="offsets")
-        pool_scales = keep.tile([P, T], U8, name="pool_scales", tag="shared2", align_bytes=64)
-        nc.vector.memset(pool_scales[:, : T // 2].bitcast(I32), 0)
-        nc.gpsimd.memset(pool_scales[:, T // 2 :].bitcast(I32), 0)
-        wk_raw = keep.tile([P, PACK, F], F32, name="wk_raw", tag="shared1", align_bytes=64)
+        pool_scales = keep.tile([P, T], U8, name="pool_scales", tag=AFTER_SCALE_GATHER, align_bytes=64)
+        nc.vector.memset(pool_scales[:].bitcast(I32), 0)
+
+        wk_raw = keep.tile([P, PACK, F], F32, name="wk_raw", tag=AFTER_WK_CAST, align_bytes=64)
         wk_rows = wk.rearrange("(p j) f -> p (j f)", j=PACK)
         wk_flat = wk_raw[:].rearrange("p j f -> p (j f)")
         nc.sync.dma_start(wk_flat[:, :WK_FIRST], wk_rows[:, :WK_FIRST])
         nc.sync.dma_start(offsets[:], offs)
-        nc.sync.dma_start(pool_scales[0:P:8, :].bitcast(I32), enc_scales[0].bitcast(I32))
+        nc.sync.dma_start(pool_scales[0:P:ROW_STEP, :].bitcast(I32), enc_scales[0].bitcast(I32))
         nc.sync.dma_start(wk_flat[:, WK_FIRST:], wk_rows[:, WK_FIRST:])
+
         warm = keep.tile([P, 1], F32, name="warm")
         nc.vector.memset(warm[:], 0.0)
         warm_out = keep.tile([P, 1], F32, name="warm_out")
@@ -51,13 +58,17 @@ def tile_attend_additiveattn_kernel(tc, enc_words, enc_scales, wk, qterm, gain, 
 
         pool_words = keep.tile([P, T], I32, name="pool_words", align_bytes=64)
         nc.sync.dma_start(pool_words[:], enc_words[0].rearrange("p n r -> p (n r)").bitcast(I32))
+
         picked_sc = keep.tile([P, I], U8, name="picked_sc", align_bytes=64)
         nc.vector.tensor_copy(picked_sc[:], pool_scales[:].indirect(offsets[:]))
         enc_sc = keep.tile([P, I], U8, name="enc_sc", align_bytes=64)
         nc.vector.tensor_copy(enc_sc[:].bitcast(I32), picked_sc[:].bitcast(I32))
         for r in range(1, 4):
-            nc.sync.dma_start(enc_sc[r:P:32, :].bitcast(I32), picked_sc[8 * r : P : 32, :].bitcast(I32))
-        late = keep.tile([P, PACK * M + 16], F32, name="late", tag="shared2", align_bytes=64)
+            nc.sync.dma_start(
+                enc_sc[r:P:QUADRANT, :].bitcast(I32), picked_sc[ROW_STEP * r : P : QUADRANT, :].bitcast(I32)
+            )
+
+        late = keep.tile([P, PACK * M + 16], F32, name="late", tag=AFTER_SCALE_GATHER, align_bytes=64)
         q_cols = late[:, PACK * M : PACK * M + PACK]
         nc.sync.dma_start(q_cols, qterm.rearrange("(p t) o -> p (t o)", t=PACK))
         score_raw = late[:, : PACK * M].rearrange("p (j m) -> p j m", j=PACK)
@@ -65,8 +76,7 @@ def tile_attend_additiveattn_kernel(tc, enc_words, enc_scales, wk, qterm, gain, 
         gain_cols = late[:, PACK * M + 8 : PACK * M + 8 + PACK]
         nc.sync.dma_start(gain_cols, gain.rearrange("(p t) o -> p (t o)", t=PACK))
 
-
-        wk_bf = keep.tile([P, PACK, P, PACK], BF16, name="wk_bf", tag="shared0", align_bytes=64)
+        wk_bf = keep.tile([P, PACK, P, PACK], BF16, name="wk_bf", tag=AFTER_WK_QUANTISER, align_bytes=64)
         src = wk_raw[:].rearrange("p j (m t) -> p m j t", t=PACK)
         dst = wk_bf[:].rearrange("p t m j -> p m j t")
         nc.vector.tensor_copy(dst[:, :WK_VECTOR_COLS], src[:, :WK_VECTOR_COLS])
@@ -78,8 +88,8 @@ def tile_attend_additiveattn_kernel(tc, enc_words, enc_scales, wk, qterm, gain, 
         )
 
         enc_codes = []
-        for g in range(I // GATHER):
-            picked = keep.tile([P, GATHER], U32, name=f"enc_codes{g}", tag=f"shared{1 - g}", align_bytes=64)
+        for g, tag in enumerate((AFTER_WK_CAST, AFTER_WK_QUANTISER)):
+            picked = keep.tile([P, GATHER], U32, name=f"enc_codes{g}", tag=tag, align_bytes=64)
             nc.vector.tensor_copy(
                 picked[:],
                 pool_words[:].bitcast(U32).indirect(offsets[:, g * GATHER // 16 : (g + 1) * GATHER // 16]),
@@ -88,44 +98,43 @@ def tile_attend_additiveattn_kernel(tc, enc_words, enc_scales, wk, qterm, gain, 
 
         score_bf = keep.tile([P, M, PACK], BF16, name="score_bf", align_bytes=64)
         nc.vector.tensor_copy(
-            score_bf[:].rearrange("p (a b) j -> p a j b", b=4),
-            score_raw.rearrange("p j (a b) -> p a j b", b=4),
+            score_bf[:].rearrange("p (a b) j -> p a j b", b=RUN),
+            score_raw.rearrange("p j (a b) -> p a j b", b=RUN),
         )
         score_codes = keep.tile([P, M], U32, name="score_codes", align_bytes=64)
         score_sc = keep.tile([P, M], U8, name="score_sc", align_bytes=64)
         nc.vector.quantize_mx(score_codes[:].bitcast(FP8X4), score_sc[:], score_bf[:].rearrange("p m j -> p (m j)"))
 
-        starts = [sum(PIECES[:n]) for n in range(len(PIECES))]
-        th = [keep.tile([P, PACK, w], F32, name=f"th{n}") for n, w in enumerate(PIECES)]
-        chunks = I // CHUNK
-        h_bf = [keep.tile([P, CHUNK, PACK], BF16, name=f"h_bf{c}", tag=f"h_bf{c}", align_bytes=64) for c in range(chunks)]
-        h_codes = [keep.tile([P, CHUNK], U32, name=f"h_codes{c}", align_bytes=64) for c in range(chunks)]
-        h_sc = [keep.tile([P, CHUNK], U8, name=f"h_sc{c}", align_bytes=64) for c in range(chunks)]
-        early = I // 2
-        logits_a = apool.tile([P, early], F32, name="logits_a")
-        logits_b = apool.tile([P, I - early], F32, name="logits_b")
+        th = [keep.tile([P, PACK, CHUNK], F32, name=f"th{c}") for c in range(CHUNKS)]
+        h_bf = [keep.tile([P, CHUNK, PACK], BF16, name=f"h_bf{c}", tag=f"h_bf{c}", align_bytes=64) for c in range(CHUNKS)]
+        h_codes = [keep.tile([P, CHUNK], U32, name=f"h_codes{c}", align_bytes=64) for c in range(CHUNKS)]
+        h_sc = [keep.tile([P, CHUNK], U8, name=f"h_sc{c}", align_bytes=64) for c in range(CHUNKS)]
+        half = I // 2
+        logits_a = apool.tile([P, half], F32, name="logits_a")
+        logits_b = apool.tile([P, half], F32, name="logits_b")
 
-        for n, (i0, w) in enumerate(zip(starts, PIECES)):
-            picked = enc_codes[i0 // GATHER][:, i0 % GATHER : i0 % GATHER + w]
+        for c in range(CHUNKS):
+            i0 = c * CHUNK
+            states = enc_codes[i0 // GATHER][:, i0 % GATHER : i0 % GATHER + CHUNK]
             for t in range(PACK):
-                rows = slice(t * P, (t + 1) * P)
-                z = zpool.tile([P, w], F32, name="z")
+                cols = slice(t * P, (t + 1) * P)
+                z = zpool.tile([P, CHUNK], F32, name="z")
                 nc.tensor.matmul_mx(
-                    z[:], lhsT=wk_codes[:, rows].bitcast(FP8X4), lhsT_scale=wk_sc[:, rows],
-                    rhs=picked.bitcast(FP8X4), rhs_scale=enc_sc[:, i0 : i0 + w], start=True, stop=True,
+                    z[:], lhsT=wk_codes[:, cols].bitcast(FP8X4), lhsT_scale=wk_sc[:, cols],
+                    rhs=states.bitcast(FP8X4), rhs_scale=enc_sc[:, i0 : i0 + CHUNK], start=True, stop=True,
                 )
-                nc.scalar.activation(th[n][:, t, :], z[:], ACT.Tanh, bias=q_cols[:, t : t + 1])
+                nc.scalar.activation(th[c][:, t, :], z[:], ACT.Tanh, bias=q_cols[:, t : t + 1])
 
-        def apply_gain(n):
-            i0, w = starts[n], PIECES[n]
-            if n == len(PIECES) - 1:
-                w = w - LAST_SCALAR_SLOTS
+        def apply_gain(c):
+            w = CHUNK
+            if c == CHUNKS - 1:
+                w = CHUNK - LAST_SCALAR_SLOTS
                 for t in range(PACK):
-                    nc.scalar.activation(h_bf[n][:, w:, t], th[n][:, t, w:], ACT.Copy, scale=gain_cols[:, t : t + 1])
+                    nc.scalar.activation(h_bf[c][:, w:, t], th[c][:, t, w:], ACT.Copy, scale=gain_cols[:, t : t + 1])
             nc.vector.tensor_tensor(
-                h_bf[i0 // CHUNK][:, i0 % CHUNK : i0 % CHUNK + w].rearrange("p (a b) t -> p a t b", b=4),
-                th[n][:, :, :w].rearrange("p t (a b) -> p a t b", b=4),
-                gain_cols.rearrange("p (a t b) -> p a t b", a=1, b=1).to_broadcast([P, w // 4, PACK, 4]),
+                h_bf[c][:, :w].rearrange("p (a b) t -> p a t b", b=RUN),
+                th[c][:, :, :w].rearrange("p t (a b) -> p a t b", b=RUN),
+                gain_cols.rearrange("p (a t b) -> p a t b", a=1, b=1).to_broadcast([P, w // RUN, PACK, RUN]),
                 ALU.mult,
             )
 
@@ -133,21 +142,23 @@ def tile_attend_additiveattn_kernel(tc, enc_words, enc_scales, wk, qterm, gain, 
             nc.vector.quantize_mx(h_codes[c][:].bitcast(FP8X4), h_sc[c][:], h_bf[c][:].rearrange("p i t -> p (i t)"))
 
         apply_gain(0)
-        for c in range(1, chunks):
+        for c in range(1, CHUNKS):
             apply_gain(c)
             quantize_h(c - 1)
-        quantize_h(chunks - 1)
-        for c in range(chunks):
+        quantize_h(CHUNKS - 1)
+        for c in range(CHUNKS):
             nc.tensor.matmul_mx(
-                (logits_a, logits_b)[c // 2][:, c % 2 * CHUNK : (c % 2 + 1) * CHUNK], lhsT=score_codes[:].bitcast(FP8X4), lhsT_scale=score_sc[:],
+                (logits_a, logits_b)[c // 2][:, c % 2 * CHUNK : (c % 2 + 1) * CHUNK],
+                lhsT=score_codes[:].bitcast(FP8X4), lhsT_scale=score_sc[:],
                 rhs=h_codes[c][:].bitcast(FP8X4), rhs_scale=h_sc[c][:], start=True, stop=True,
             )
 
-        neg_logits = keep.tile([P, I], F32, name="neg_logits", tag=f"h_bf{chunks - 2}", align_bytes=64)
+        neg_logits = keep.tile([P, I], F32, name="neg_logits", tag=f"h_bf{CHUNKS - 2}", align_bytes=64)
         neg_max_a = keep.tile([P, 1], F32, name="neg_max_a")
-        nc.vector.tensor_scalar(neg_logits[:, :early], logits_a[:], -1.0, None, ALU.mult, ALU.min, accum_out=neg_max_a[:])
+        nc.vector.tensor_scalar(neg_logits[:, :half], logits_a[:], -1.0, None, ALU.mult, ALU.min, accum_out=neg_max_a[:])
         neg_max = keep.tile([P, 1], F32, name="neg_max")
-        nc.vector.tensor_scalar(neg_logits[:, early:], logits_b[:], -1.0, neg_max_a[:], ALU.mult, ALU.min, accum_out=neg_max[:])
+        nc.vector.tensor_scalar(neg_logits[:, half:], logits_b[:], -1.0, neg_max_a[:], ALU.mult, ALU.min, accum_out=neg_max[:])
+
         p_exp = keep.tile([P, I], F32, name="p_exp")
         row_sum = keep.tile([P, 1], F32, name="row_sum")
         nc.scalar.activation(p_exp[:], neg_logits[:], ACT.Exp, bias=neg_max[:], scale=-1.0, accum_out=row_sum[:])

@@ -25,7 +25,7 @@ CHUNKS = I // CHUNK
 GATHER = 256
 Z_BANKS = 6
 WK_FIRST = 768
-WK_VECTOR_COLS = 80
+WK_VECTOR_COLS = 24
 LAST_SCALAR_SLOTS = 32
 AFTER_WK_QUANTISER = "shared0"
 AFTER_WK_CAST = "shared1"
@@ -76,16 +76,21 @@ def tile_attend_additiveattn_kernel(tc, enc_words, enc_scales, wk, qterm, gain, 
         gain_cols = late[:, PACK * M + 8 : PACK * M + 8 + PACK]
         nc.sync.dma_start(gain_cols, gain.rearrange("(p t) o -> p (t o)", t=PACK))
 
-        wk_bf = keep.tile([P, PACK, P, PACK], BF16, name="wk_bf", tag=AFTER_WK_QUANTISER, align_bytes=64)
+        wk_bf = [
+            keep.tile([P, 2, P, PACK], BF16, name=f"wk_bf{u}", tag=tag, align_bytes=64)
+            for u, tag in enumerate(("wk_bf0", AFTER_WK_QUANTISER))
+        ]
         src = wk_raw[:].rearrange("p j (m t) -> p m j t", t=PACK)
-        dst = wk_bf[:].rearrange("p t m j -> p m j t")
-        nc.vector.tensor_copy(dst[:, :WK_VECTOR_COLS], src[:, :WK_VECTOR_COLS])
-        nc.scalar.activation(dst[:, WK_VECTOR_COLS:], src[:, WK_VECTOR_COLS:], ACT.Copy)
-        wk_codes = keep.tile([P, F], U32, name="wk_codes", align_bytes=64)
-        wk_sc = keep.tile([P, F], U8, name="wk_sc", align_bytes=64)
-        nc.vector.quantize_mx(
-            wk_codes[:].bitcast(FP8X4), wk_sc[:], wk_bf[:].rearrange("p t m j -> p (t m j)")
-        )
+        dst = [wk_bf[u][:].rearrange("p e m j -> p m j e") for u in range(2)]
+        nc.vector.tensor_copy(dst[0], src[:, :, :, :2])
+        nc.vector.tensor_copy(dst[1][:, :WK_VECTOR_COLS], src[:, :WK_VECTOR_COLS, :, 2:])
+        nc.scalar.activation(dst[1][:, WK_VECTOR_COLS:], src[:, WK_VECTOR_COLS:, :, 2:], ACT.Copy)
+        wk_codes = [keep.tile([P, 2 * P], U32, name=f"wk_codes{u}", align_bytes=64) for u in range(2)]
+        wk_sc = [keep.tile([P, 2 * P], U8, name=f"wk_sc{u}", align_bytes=64) for u in range(2)]
+        for u in range(2):
+            nc.vector.quantize_mx(
+                wk_codes[u][:].bitcast(FP8X4), wk_sc[u][:], wk_bf[u][:].rearrange("p e m j -> p (e m j)")
+            )
 
         enc_codes = []
         for g, tag in enumerate((AFTER_WK_CAST, AFTER_WK_QUANTISER)):
@@ -96,14 +101,19 @@ def tile_attend_additiveattn_kernel(tc, enc_words, enc_scales, wk, qterm, gain, 
             )
             enc_codes.append(picked)
 
-        score_bf = keep.tile([P, M, PACK], BF16, name="score_bf", align_bytes=64)
-        nc.vector.tensor_copy(
-            score_bf[:].rearrange("p (a b) j -> p a j b", b=RUN),
-            score_raw.rearrange("p j (a b) -> p a j b", b=RUN),
-        )
+        score_bf = [keep.tile([P, M // 2, PACK], BF16, name=f"score_bf{h}", align_bytes=64) for h in range(2)]
         score_codes = keep.tile([P, M], U32, name="score_codes", align_bytes=64)
         score_sc = keep.tile([P, M], U8, name="score_sc", align_bytes=64)
-        nc.vector.quantize_mx(score_codes[:].bitcast(FP8X4), score_sc[:], score_bf[:].rearrange("p m j -> p (m j)"))
+        for h in range(2):
+            nc.vector.tensor_copy(
+                score_bf[h][:].rearrange("p (a b) j -> p a j b", b=RUN),
+                score_raw[:, :, h * M // 2 : (h + 1) * M // 2].rearrange("p j (a b) -> p a j b", b=RUN),
+            )
+        for h in range(2):
+            heads = slice(h * M // 2, (h + 1) * M // 2)
+            nc.vector.quantize_mx(
+                score_codes[:, heads].bitcast(FP8X4), score_sc[:, heads], score_bf[h][:].rearrange("p m j -> p (m j)")
+            )
 
         th = [keep.tile([P, PACK, CHUNK], F32, name=f"th{c}") for c in range(CHUNKS)]
         h_bf = [keep.tile([P, CHUNK, PACK], BF16, name=f"h_bf{c}", tag=f"h_bf{c}", align_bytes=64) for c in range(CHUNKS)]
@@ -117,10 +127,10 @@ def tile_attend_additiveattn_kernel(tc, enc_words, enc_scales, wk, qterm, gain, 
             i0 = c * CHUNK
             states = enc_codes[i0 // GATHER][:, i0 % GATHER : i0 % GATHER + CHUNK]
             for t in range(PACK):
-                cols = slice(t * P, (t + 1) * P)
+                cols = slice(t % 2 * P, (t % 2 + 1) * P)
                 z = zpool.tile([P, CHUNK], F32, name="z")
                 nc.tensor.matmul_mx(
-                    z[:], lhsT=wk_codes[:, cols].bitcast(FP8X4), lhsT_scale=wk_sc[:, cols],
+                    z[:], lhsT=wk_codes[t // 2][:, cols].bitcast(FP8X4), lhsT_scale=wk_sc[t // 2][:, cols],
                     rhs=states.bitcast(FP8X4), rhs_scale=enc_sc[:, i0 : i0 + CHUNK], start=True, stop=True,
                 )
                 nc.scalar.activation(th[c][:, t, :], z[:], ACT.Tanh, bias=q_cols[:, t : t + 1])

@@ -68,12 +68,12 @@ def tile_attend_additiveattn_kernel(tc, enc_words, enc_scales, wk, qterm, gain, 
                 enc_sc[r:P:QUADRANT, :].bitcast(I32), picked_sc[ROW_STEP * r : P : QUADRANT, :].bitcast(I32)
             )
 
-        late = keep.tile([P, PACK * M + 16], F32, name="late", tag=AFTER_SCALE_GATHER, align_bytes=64)
-        q_cols = late[:, PACK * M : PACK * M + PACK]
-        nc.sync.dma_start(q_cols, qterm.rearrange("(p t) o -> p (t o)", t=PACK))
-        score_raw = late[:, : PACK * M].rearrange("p (j m) -> p j m", j=PACK)
-        nc.sync.dma_start(score_raw, score.rearrange("(p j) m -> p j m", j=PACK))
-        gain_cols = late[:, PACK * M + 8 : PACK * M + 8 + PACK]
+        q_cols = keep.tile([P, PACK], F32, name="q_cols")
+        nc.sync.dma_start(q_cols[:], qterm.rearrange("(p t) o -> p (t o)", t=PACK))
+        score_raw = keep.tile([P, PACK, M], F32, name="score_raw", align_bytes=64)
+        nc.sync.dma_start(score_raw[:], score.rearrange("(p j) m -> p j m", j=PACK))
+        gain_tile = keep.tile([P, PACK], F32, name="gain_tile", tag=AFTER_SCALE_GATHER, align_bytes=64)
+        gain_cols = gain_tile[:]
         nc.sync.dma_start(gain_cols, gain.rearrange("(p t) o -> p (t o)", t=PACK))
 
         wk_bf = [

@@ -23,8 +23,8 @@ RUN = 4
 CHUNK = 128
 CHUNKS = I // CHUNK
 GATHER = 256
-Z_BANKS = 6
-WK_FIRST = 768
+Z_BANKS = 8
+WK_FIRST = 1024
 WK_VECTOR_COLS = 24
 LAST_SCALAR_SLOTS = 32
 AFTER_WK_QUANTISER = "shared0"
@@ -37,7 +37,6 @@ def tile_attend_additiveattn_kernel(tc, enc_words, enc_scales, wk, qterm, gain, 
     with ExitStack() as ctx:
         keep = ctx.enter_context(tc.tile_pool(name="keep", bufs=1))
         zpool = ctx.enter_context(tc.psum_pool(name="zpool", bufs=Z_BANKS))
-        apool = ctx.enter_context(tc.psum_pool(name="apool", bufs=1))
 
         offsets = keep.tile([P, I // 16], U16, name="offsets")
         pool_scales = keep.tile([P, T], U8, name="pool_scales", tag=AFTER_SCALE_GATHER, align_bytes=64)
@@ -120,8 +119,6 @@ def tile_attend_additiveattn_kernel(tc, enc_words, enc_scales, wk, qterm, gain, 
         h_codes = [keep.tile([P, CHUNK], U32, name=f"h_codes{c}", align_bytes=64) for c in range(CHUNKS)]
         h_sc = [keep.tile([P, CHUNK], U8, name=f"h_sc{c}", align_bytes=64) for c in range(CHUNKS)]
         half = I // 2
-        logits_a = apool.tile([P, half], F32, name="logits_a")
-        logits_b = apool.tile([P, half], F32, name="logits_b")
 
         for c in range(CHUNKS):
             i0 = c * CHUNK
@@ -150,6 +147,9 @@ def tile_attend_additiveattn_kernel(tc, enc_words, enc_scales, wk, qterm, gain, 
 
         def quantize_h(c):
             nc.vector.quantize_mx(h_codes[c][:].bitcast(FP8X4), h_sc[c][:], h_bf[c][:].rearrange("p i t -> p (i t)"))
+
+        logits_a = zpool.tile([P, half], F32, name="logits_a", tag="z")
+        logits_b = zpool.tile([P, half], F32, name="logits_b", tag="z")
 
         apply_gain(0)
         for c in range(1, CHUNKS):

@@ -25,8 +25,8 @@ CHUNKS = I // CHUNK
 GATHER = 256
 Z_BANKS = 8
 WK_FIRST = 1024
-WK_VECTOR_COLS = 24
-LAST_SCALAR_SLOTS = 32
+WK_VECTOR_COLS = 72
+LAST_SCALAR_SLOTS = 64
 AFTER_WK_QUANTISER = "shared0"
 AFTER_WK_CAST = "shared1"
 AFTER_SCALE_GATHER = "shared2"
@@ -81,9 +81,10 @@ def tile_attend_additiveattn_kernel(tc, enc_words, enc_scales, wk, qterm, gain, 
         ]
         src = wk_raw[:].rearrange("p j (m t) -> p m j t", t=PACK)
         dst = [wk_bf[u][:].rearrange("p e m j -> p m j e") for u in range(2)]
-        nc.vector.tensor_copy(dst[0], src[:, :, :, :2])
-        nc.vector.tensor_copy(dst[1][:, :WK_VECTOR_COLS], src[:, :WK_VECTOR_COLS, :, 2:])
-        nc.scalar.activation(dst[1][:, WK_VECTOR_COLS:], src[:, WK_VECTOR_COLS:, :, 2:], ACT.Copy)
+        for u in range(2):
+            pair = src[:, :, :, 2 * u : 2 * u + 2]
+            nc.vector.tensor_copy(dst[u][:, :WK_VECTOR_COLS], pair[:, :WK_VECTOR_COLS])
+            nc.scalar.activation(dst[u][:, WK_VECTOR_COLS:], pair[:, WK_VECTOR_COLS:], ACT.Copy)
         wk_codes = [keep.tile([P, 2 * P], U32, name=f"wk_codes{u}", align_bytes=64) for u in range(2)]
         wk_sc = [keep.tile([P, 2 * P], U8, name=f"wk_sc{u}", align_bytes=64) for u in range(2)]
         for u in range(2):

@@ -26,7 +26,7 @@ GATHER = 256
 Z_BANKS = 8
 WK_FIRST = 1024
 WK_VECTOR_COLS = 72
-LAST_SCALAR_SLOTS = 64
+LAST_SCALAR_SLOTS = 56
 AFTER_WK_QUANTISER = "shared0"
 AFTER_WK_CAST = "shared1"
 AFTER_SCALE_GATHER = "shared2"
@@ -58,6 +58,11 @@ def tile_attend_additiveattn_kernel(tc, enc_words, enc_scales, wk, qterm, gain, 
         pool_words = keep.tile([P, T], I32, name="pool_words", align_bytes=64)
         nc.sync.dma_start(pool_words[:], enc_words[0].rearrange("p n r -> p (n r)").bitcast(I32))
 
+        q_cols = keep.tile([P, PACK], F32, name="q_cols")
+        nc.sync.dma_start(q_cols[:], qterm.rearrange("(p t) o -> p (t o)", t=PACK))
+        score_raw = keep.tile([P, PACK, M], F32, name="score_raw", align_bytes=64)
+        nc.sync.dma_start(score_raw[:], score.rearrange("(p j) m -> p j m", j=PACK))
+
         picked_sc = keep.tile([P, I], U8, name="picked_sc", align_bytes=64)
         nc.vector.tensor_copy(picked_sc[:], pool_scales[:].indirect(offsets[:]))
         enc_sc = keep.tile([P, I], U8, name="enc_sc", align_bytes=64)
@@ -67,10 +72,6 @@ def tile_attend_additiveattn_kernel(tc, enc_words, enc_scales, wk, qterm, gain, 
                 enc_sc[r:P:QUADRANT, :].bitcast(I32), picked_sc[ROW_STEP * r : P : QUADRANT, :].bitcast(I32)
             )
 
-        q_cols = keep.tile([P, PACK], F32, name="q_cols")
-        nc.sync.dma_start(q_cols[:], qterm.rearrange("(p t) o -> p (t o)", t=PACK))
-        score_raw = keep.tile([P, PACK, M], F32, name="score_raw", align_bytes=64)
-        nc.sync.dma_start(score_raw[:], score.rearrange("(p j) m -> p j m", j=PACK))
         gain_tile = keep.tile([P, PACK], F32, name="gain_tile", tag=AFTER_SCALE_GATHER, align_bytes=64)
         gain_cols = gain_tile[:]
         nc.sync.dma_start(gain_cols, gain.rearrange("(p t) o -> p (t o)", t=PACK))

@@ -18,13 +18,13 @@ ALU = mybir.AluOpType
 P = 128
 PACK = 4
 QUADRANT = 32
-ROW_STEP = 8
+ROW_FIRST, ROW_STEP = 32, 4
 RUN = 4
 CHUNK = 128
 CHUNKS = I // CHUNK
 GATHER = 256
 Z_BANKS = 8
-WK_FIRST = 1024
+WK_FIRST = 896
 WK_VECTOR_COLS = 72
 LAST_SCALAR_SLOTS = 56
 AFTER_WK_QUANTISER = "shared0"
@@ -47,9 +47,11 @@ def tile_attend_additiveattn_kernel(tc, enc_words, enc_scales, wk, qterm, gain, 
         wk_flat = wk_raw[:].rearrange("p j f -> p (j f)")
         nc.sync.dma_start(wk_flat[:, :WK_FIRST], wk_rows[:, :WK_FIRST])
         nc.sync.dma_start(offsets[:], offs)
-        nc.sync.dma_start(pool_scales[0:P:ROW_STEP, :].bitcast(I32), enc_scales[0].bitcast(I32))
+        nc.sync.dma_start(pool_scales[ROW_FIRST : ROW_FIRST + 16 * ROW_STEP : ROW_STEP, :].bitcast(I32), enc_scales[0].bitcast(I32))
         nc.sync.dma_start(wk_flat[:, WK_FIRST:], wk_rows[:, WK_FIRST:])
 
+        enc_sc = keep.tile([P, I], U8, name="enc_sc", align_bytes=64)
+        nc.vector.memset(enc_sc[:].bitcast(I32), 0)
         warm = keep.tile([P, 1], F32, name="warm")
         nc.vector.memset(warm[:], 0.0)
         warm_out = keep.tile([P, 1], F32, name="warm_out")
@@ -65,11 +67,11 @@ def tile_attend_additiveattn_kernel(tc, enc_words, enc_scales, wk, qterm, gain, 
 
         picked_sc = keep.tile([P, I], U8, name="picked_sc", align_bytes=64)
         nc.vector.tensor_copy(picked_sc[:], pool_scales[:].indirect(offsets[:]))
-        enc_sc = keep.tile([P, I], U8, name="enc_sc", align_bytes=64)
-        nc.vector.tensor_copy(enc_sc[:].bitcast(I32), picked_sc[:].bitcast(I32))
-        for r in range(1, 4):
+        for r in range(4):
+            first = ROW_FIRST + ROW_STEP * r
             nc.sync.dma_start(
-                enc_sc[r:P:QUADRANT, :].bitcast(I32), picked_sc[ROW_STEP * r : P : QUADRANT, :].bitcast(I32)
+                enc_sc[r:P:QUADRANT, :].bitcast(I32),
+                picked_sc[first : first + 16 * ROW_STEP : 4 * ROW_STEP, :].bitcast(I32),
             )
 
         gain_tile = keep.tile([P, PACK], F32, name="gain_tile", tag=AFTER_SCALE_GATHER, align_bytes=64)

@@ -22,14 +22,12 @@ ROW_FIRST, ROW_STEP = 32, 4
 RUN = 4
 CHUNK = 128
 CHUNKS = I // CHUNK
-GATHER = 256
 Z_BANKS = 8
 WK_FIRST = 896
 WK_VECTOR_COLS = 72
 LAST_SCALAR_SLOTS = 56
 AFTER_WK_QUANTISER = "shared0"
-AFTER_WK_CAST = "shared1"
-AFTER_SCALE_GATHER = "shared2"
+AFTER_SCALE_GATHER = "shared1"
 
 
 def tile_attend_additiveattn_kernel(tc, enc_words, enc_scales, wk, qterm, gain, score, offs, out):
@@ -42,7 +40,7 @@ def tile_attend_additiveattn_kernel(tc, enc_words, enc_scales, wk, qterm, gain, 
         pool_scales = keep.tile([P, T], U8, name="pool_scales", tag=AFTER_SCALE_GATHER, align_bytes=64)
         nc.vector.memset(pool_scales[:].bitcast(I32), 0)
 
-        wk_raw = keep.tile([P, PACK, F], F32, name="wk_raw", tag=AFTER_WK_CAST, align_bytes=64)
+        wk_raw = keep.tile([P, PACK, F], F32, name="wk_raw", align_bytes=64)
         wk_rows = wk.rearrange("(p j) f -> p (j f)", j=PACK)
         wk_flat = wk_raw[:].rearrange("p j f -> p (j f)")
         nc.sync.dma_start(wk_flat[:, :WK_FIRST], wk_rows[:, :WK_FIRST])
@@ -60,11 +58,6 @@ def tile_attend_additiveattn_kernel(tc, enc_words, enc_scales, wk, qterm, gain, 
         pool_words = keep.tile([P, T], I32, name="pool_words", align_bytes=64)
         nc.sync.dma_start(pool_words[:], enc_words[0].rearrange("p n r -> p (n r)").bitcast(I32))
 
-        q_cols = keep.tile([P, PACK], F32, name="q_cols")
-        nc.sync.dma_start(q_cols[:], qterm.rearrange("(p t) o -> p (t o)", t=PACK))
-        score_raw = keep.tile([P, PACK, M], F32, name="score_raw", align_bytes=64)
-        nc.sync.dma_start(score_raw[:], score.rearrange("(p j) m -> p j m", j=PACK))
-
         picked_sc = keep.tile([P, I], U8, name="picked_sc", align_bytes=64)
         nc.vector.tensor_copy(picked_sc[:], pool_scales[:].indirect(offsets[:]))
         for r in range(4):
@@ -74,8 +67,12 @@ def tile_attend_additiveattn_kernel(tc, enc_words, enc_scales, wk, qterm, gain, 
                 picked_sc[first : first + 16 * ROW_STEP : 4 * ROW_STEP, :].bitcast(I32),
             )
 
-        gain_tile = keep.tile([P, PACK], F32, name="gain_tile", tag=AFTER_SCALE_GATHER, align_bytes=64)
-        gain_cols = gain_tile[:]
+        late = keep.tile([P, PACK * M + 4 * PACK], F32, name="late", tag=AFTER_SCALE_GATHER, align_bytes=64)
+        score_raw = late[:, : PACK * M]
+        q_cols = late[:, PACK * M : PACK * M + PACK]
+        gain_cols = late[:, PACK * M + 2 * PACK : PACK * M + 3 * PACK]
+        nc.sync.dma_start(q_cols, qterm.rearrange("(p t) o -> p (t o)", t=PACK))
+        nc.sync.dma_start(score_raw, score.rearrange("(p j) m -> p (j m)", j=PACK))
         nc.sync.dma_start(gain_cols, gain.rearrange("(p t) o -> p (t o)", t=PACK))
 
         wk_bf = [
@@ -95,14 +92,12 @@ def tile_attend_additiveattn_kernel(tc, enc_words, enc_scales, wk, qterm, gain, 
                 wk_codes[u][:].bitcast(FP8X4), wk_sc[u][:], wk_bf[u][:].rearrange("p e m j -> p (e m j)")
             )
 
-        enc_codes = []
-        for g, tag in enumerate((AFTER_WK_CAST, AFTER_WK_QUANTISER)):
-            picked = keep.tile([P, GATHER], U32, name=f"enc_codes{g}", tag=tag, align_bytes=64)
+        enc_codes = keep.tile([P, I], U32, name="enc_codes", tag=AFTER_WK_QUANTISER, align_bytes=64)
+        for c in range(CHUNKS):
             nc.vector.tensor_copy(
-                picked[:],
-                pool_words[:].bitcast(U32).indirect(offsets[:, g * GATHER // 16 : (g + 1) * GATHER // 16]),
+                enc_codes[:, c * CHUNK : (c + 1) * CHUNK],
+                pool_words[:].bitcast(U32).indirect(offsets[:, c * CHUNK // 16 : (c + 1) * CHUNK // 16]),
             )
-            enc_codes.append(picked)
 
         score_bf = [keep.tile([P, M // 2, PACK], BF16, name=f"score_bf{h}", align_bytes=64) for h in range(2)]
         score_codes = keep.tile([P, M], U32, name="score_codes", align_bytes=64)
@@ -110,7 +105,7 @@ def tile_attend_additiveattn_kernel(tc, enc_words, enc_scales, wk, qterm, gain, 
         for h in range(2):
             nc.vector.tensor_copy(
                 score_bf[h][:].rearrange("p (a b) j -> p a j b", b=RUN),
-                score_raw[:, :, h * M // 2 : (h + 1) * M // 2].rearrange("p j (a b) -> p a j b", b=RUN),
+                score_raw.rearrange("p (j a b) -> p a j b", j=PACK, b=RUN)[:, h * M // (2 * RUN) : (h + 1) * M // (2 * RUN)],
             )
         for h in range(2):
             heads = slice(h * M // 2, (h + 1) * M // 2)
@@ -126,7 +121,7 @@ def tile_attend_additiveattn_kernel(tc, enc_words, enc_scales, wk, qterm, gain, 
 
         for c in range(CHUNKS):
             i0 = c * CHUNK
-            states = enc_codes[i0 // GATHER][:, i0 % GATHER : i0 % GATHER + CHUNK]
+            states = enc_codes[:, i0 : i0 + CHUNK]
             for t in range(PACK):
                 cols = slice(t % 2 * P, (t % 2 + 1) * P)
                 z = zpool.tile([P, CHUNK], F32, name="z")

@@ -25,7 +25,7 @@ CHUNKS = I // CHUNK
 Z_BANKS = 8
 WK_FIRST = 896
 WK_VECTOR_COLS = 72
-LAST_SCALAR_SLOTS = 56
+LAST_SCALAR_SLOTS = 60
 AFTER_WK_QUANTISER = "shared0"
 AFTER_SCALE_GATHER = "shared1"
 

@@ -19,6 +19,7 @@ P = 128
 PACK = 4
 QUADRANT = 32
 ROW_FIRST, ROW_STEP = 32, 4
+BURST = 256
 RUN = 4
 CHUNK = 128
 CHUNKS = I // CHUNK
@@ -37,10 +38,10 @@ def tile_attend_additiveattn_kernel(tc, enc_words, enc_scales, wk, qterm, gain, 
         zpool = ctx.enter_context(tc.psum_pool(name="zpool", bufs=Z_BANKS))
 
         offsets = keep.tile([P, I // 16], U16, name="offsets")
-        pool_scales = keep.tile([P, T], U8, name="pool_scales", tag=AFTER_SCALE_GATHER, align_bytes=64)
+        pool_scales = keep.tile([P, T], U8, name="pool_scales", tag=AFTER_SCALE_GATHER, align_bytes=BURST)
         nc.vector.memset(pool_scales[:].bitcast(I32), 0)
 
-        wk_raw = keep.tile([P, PACK, F], F32, name="wk_raw", align_bytes=64)
+        wk_raw = keep.tile([P, PACK, F], F32, name="wk_raw", align_bytes=BURST)
         wk_rows = wk.rearrange("(p j) f -> p (j f)", j=PACK)
         wk_flat = wk_raw[:].rearrange("p j f -> p (j f)")
         nc.sync.dma_start(wk_flat[:, :WK_FIRST], wk_rows[:, :WK_FIRST])
@@ -48,17 +49,17 @@ def tile_attend_additiveattn_kernel(tc, enc_words, enc_scales, wk, qterm, gain, 
         nc.sync.dma_start(pool_scales[ROW_FIRST : ROW_FIRST + 16 * ROW_STEP : ROW_STEP, :].bitcast(I32), enc_scales[0].bitcast(I32))
         nc.sync.dma_start(wk_flat[:, WK_FIRST:], wk_rows[:, WK_FIRST:])
 
-        enc_sc = keep.tile([P, I], U8, name="enc_sc", align_bytes=64)
+        enc_sc = keep.tile([P, I], U8, name="enc_sc", align_bytes=BURST)
         nc.vector.memset(enc_sc[:].bitcast(I32), 0)
         warm = keep.tile([P, 1], F32, name="warm")
         nc.vector.memset(warm[:], 0.0)
         warm_out = keep.tile([P, 1], F32, name="warm_out")
         nc.scalar.activation(warm_out[:], warm[:], ACT.Exp)
 
-        pool_words = keep.tile([P, T], I32, name="pool_words", align_bytes=64)
+        pool_words = keep.tile([P, T], I32, name="pool_words", align_bytes=BURST)
         nc.sync.dma_start(pool_words[:], enc_words[0].rearrange("p n r -> p (n r)").bitcast(I32))
 
-        picked_sc = keep.tile([P, I], U8, name="picked_sc", align_bytes=64)
+        picked_sc = keep.tile([P, I], U8, name="picked_sc", align_bytes=BURST)
         nc.vector.tensor_copy(picked_sc[:], pool_scales[:].indirect(offsets[:]))
         for r in range(4):
             first = ROW_FIRST + ROW_STEP * r
@@ -67,7 +68,7 @@ def tile_attend_additiveattn_kernel(tc, enc_words, enc_scales, wk, qterm, gain, 
                 picked_sc[first : first + 16 * ROW_STEP : 4 * ROW_STEP, :].bitcast(I32),
             )
 
-        late = keep.tile([P, PACK * M + 4 * PACK], F32, name="late", tag=AFTER_SCALE_GATHER, align_bytes=64)
+        late = keep.tile([P, PACK * M + 4 * PACK], F32, name="late", tag=AFTER_SCALE_GATHER, align_bytes=BURST)
         score_raw = late[:, : PACK * M]
         q_cols = late[:, PACK * M : PACK * M + PACK]
         gain_cols = late[:, PACK * M + 2 * PACK : PACK * M + 3 * PACK]
@@ -173,6 +174,6 @@ def tile_attend_additiveattn_kernel(tc, enc_words, enc_scales, wk, qterm, gain, 
         nc.scalar.activation(p_exp[:], neg_logits[:], ACT.Exp, bias=neg_max[:], scale=-1.0, accum_out=row_sum[:])
         inv_sum = keep.tile([P, 1], F32, name="inv_sum")
         nc.vector.reciprocal(inv_sum[:], row_sum[:])
-        result = keep.tile([P, I], F32, name="result")
+        result = keep.tile([P, I], F32, name="result", align_bytes=BURST)
         nc.vector.tensor_scalar(result[:], p_exp[:], inv_sum[:], 512.0, ALU.mult, ALU.mult)
         nc.sync.dma_start(out, result[:])

@@ -1,6 +1,7 @@
 from contextlib import ExitStack
 
 import concourse.mybir as mybir
+from concourse.masks import make_identity
 
 K, T, I, F, M = 512, 2048, 512, 512, 128
 FLOPS = 2 * K * F * I + 2 * F * M * I
@@ -23,10 +24,11 @@ BURST = 256
 RUN = 4
 CHUNK = 128
 CHUNKS = I // CHUNK
-Z_BANKS = 8
+Z_BANKS = 7
 WK_FIRST = 896
 WK_VECTOR_COLS = 72
-LAST_SCALAR_SLOTS = 60
+LAST_SCALAR_SLOTS = 44
+POOL_SLOTS = 20
 AFTER_WK_QUANTISER = "shared0"
 AFTER_SCALE_GATHER = "shared1"
 
@@ -36,6 +38,8 @@ def tile_attend_additiveattn_kernel(tc, enc_words, enc_scales, wk, qterm, gain, 
     with ExitStack() as ctx:
         keep = ctx.enter_context(tc.tile_pool(name="keep", bufs=1))
         zpool = ctx.enter_context(tc.psum_pool(name="zpool", bufs=Z_BANKS))
+
+        gpool = ctx.enter_context(tc.psum_pool(name="gpool", bufs=1))
 
         offsets = keep.tile([P, I // 16], U16, name="offsets")
         pool_scales = keep.tile([P, T], U8, name="pool_scales", tag=AFTER_SCALE_GATHER, align_bytes=BURST)
@@ -50,11 +54,18 @@ def tile_attend_additiveattn_kernel(tc, enc_words, enc_scales, wk, qterm, gain, 
         nc.sync.dma_start(wk_flat[:, WK_FIRST:], wk_rows[:, WK_FIRST:])
 
         enc_sc = keep.tile([P, I], U8, name="enc_sc", align_bytes=BURST)
-        nc.vector.memset(enc_sc[:].bitcast(I32), 0)
-        warm = keep.tile([P, 1], F32, name="warm")
-        nc.vector.memset(warm[:], 0.0)
+        nc.gpsimd.memset(enc_sc[:].bitcast(I32), 0)
+        gain_row = keep.tile([P, F + RUN], F32, name="gain_row", align_bytes=BURST)
+        nc.vector.memset(gain_row[:], 0.0)
         warm_out = keep.tile([P, 1], F32, name="warm_out")
-        nc.scalar.activation(warm_out[:], warm[:], ACT.Exp)
+        nc.scalar.activation(warm_out[:], gain_row[:, F : F + 1], ACT.Exp)
+
+        nc.sync.dma_start(gain_row[0:1, :F], gain.rearrange("f o -> o f"))
+        identity = keep.tile([P, P], F32, name="identity")
+        make_identity(nc, identity[:])
+        gain_bank = gpool.tile([P, PACK, P], F32, name="gain_bank")
+        for t in range(PACK):
+            nc.tensor.transpose(gain_bank[:, t, :], gain_row[:, t:F:PACK], identity[:])
 
         pool_words = keep.tile([P, T], I32, name="pool_words", align_bytes=BURST)
         nc.sync.dma_start(pool_words[:], enc_words[0].rearrange("p n r -> p (n r)").bitcast(I32))
@@ -94,11 +105,8 @@ def tile_attend_additiveattn_kernel(tc, enc_words, enc_scales, wk, qterm, gain, 
             )
 
         enc_codes = keep.tile([P, I], U32, name="enc_codes", tag=AFTER_WK_QUANTISER, align_bytes=64)
-        for c in range(CHUNKS):
-            nc.vector.tensor_copy(
-                enc_codes[:, c * CHUNK : (c + 1) * CHUNK],
-                pool_words[:].bitcast(U32).indirect(offsets[:, c * CHUNK // 16 : (c + 1) * CHUNK // 16]),
-            )
+        for i0, i1 in ((0, CHUNK), (CHUNK, I // 2), (I // 2, I)):
+            nc.vector.tensor_copy(enc_codes[:, i0:i1], pool_words[:].bitcast(U32).indirect(offsets[:, i0 // 16 : i1 // 16]))
 
         score_bf = [keep.tile([P, M // 2, PACK], BF16, name=f"score_bf{h}", align_bytes=64) for h in range(2)]
         score_codes = keep.tile([P, M], U32, name="score_codes", align_bytes=64)
@@ -138,10 +146,18 @@ def tile_attend_additiveattn_kernel(tc, enc_words, enc_scales, wk, qterm, gain, 
                 w = CHUNK - LAST_SCALAR_SLOTS
                 for t in range(PACK):
                     nc.scalar.activation(h_bf[c][:, w:, t], th[c][:, t, w:], ACT.Copy, scale=gain_cols[:, t : t + 1])
+            v = w - POOL_SLOTS
+            nc.gpsimd.tensor_tensor(
+                h_bf[c][:, v:w],
+                th[c][:, :, v:w].rearrange("p t i -> p i t"),
+                gain_cols.rearrange("p (i t) -> p i t", i=1).to_broadcast([P, POOL_SLOTS, PACK]),
+                ALU.mult,
+            )
+            w = v
             nc.vector.tensor_tensor(
                 h_bf[c][:, :w].rearrange("p (a b) t -> p a t b", b=RUN),
                 th[c][:, :, :w].rearrange("p t (a b) -> p a t b", b=RUN),
-                gain_cols.rearrange("p (a t b) -> p a t b", a=1, b=1).to_broadcast([P, w // RUN, PACK, RUN]),
+                gain_bank[:, :, 0:1].rearrange("p (a t) b -> p a t b", a=1).to_broadcast([P, w // RUN, PACK, RUN]),
                 ALU.mult,
             )
 

@@ -56,7 +56,7 @@ def tile_attend_additiveattn_kernel(tc, enc_words, enc_scales, wk, qterm, gain, 
         enc_sc = keep.tile([P, I], U8, name="enc_sc", align_bytes=BURST)
         nc.gpsimd.memset(enc_sc[:].bitcast(I32), 0)
         gain_row = keep.tile([P, F + RUN], F32, name="gain_row", align_bytes=BURST)
-        nc.vector.memset(gain_row[:], 0.0)
+        nc.gpsimd.memset(gain_row[:], 0.0)
         warm_out = keep.tile([P, 1], F32, name="warm_out")
         nc.scalar.activation(warm_out[:], gain_row[:, F : F + 1], ACT.Exp)
 
@@ -161,8 +161,10 @@ def tile_attend_additiveattn_kernel(tc, enc_words, enc_scales, wk, qterm, gain, 
                 ALU.mult,
             )
 
-        def quantize_h(c):
-            nc.vector.quantize_mx(h_codes[c][:].bitcast(FP8X4), h_sc[c][:], h_bf[c][:].rearrange("p i t -> p (i t)"))
+        def quantize_h(c, i0, i1):
+            nc.vector.quantize_mx(
+                h_codes[c][:, i0:i1].bitcast(FP8X4), h_sc[c][:, i0:i1], h_bf[c][:, i0:i1].rearrange("p i t -> p (i t)")
+            )
 
         logits_a = zpool.tile([P, half], F32, name="logits_a", tag="z")
         logits_b = zpool.tile([P, half], F32, name="logits_b", tag="z")
@@ -170,13 +172,15 @@ def tile_attend_additiveattn_kernel(tc, enc_words, enc_scales, wk, qterm, gain, 
         apply_gain(0)
         for c in range(1, CHUNKS):
             apply_gain(c)
-            quantize_h(c - 1)
-        quantize_h(CHUNKS - 1)
-        for c in range(CHUNKS):
+            quantize_h(c - 1, 0, CHUNK)
+        pieces = [(c, 0, CHUNK) for c in range(CHUNKS - 1)] + [(CHUNKS - 1, 0, CHUNK // 2), (CHUNKS - 1, CHUNK // 2, CHUNK)]
+        for c, i0, i1 in pieces[CHUNKS - 1 :]:
+            quantize_h(c, i0, i1)
+        for c, i0, i1 in pieces:
             nc.tensor.matmul_mx(
-                (logits_a, logits_b)[c // 2][:, c % 2 * CHUNK : (c % 2 + 1) * CHUNK],
+                (logits_a, logits_b)[c // 2][:, c % 2 * CHUNK + i0 : c % 2 * CHUNK + i1],
                 lhsT=score_codes[:].bitcast(FP8X4), lhsT_scale=score_sc[:],
-                rhs=h_codes[c][:].bitcast(FP8X4), rhs_scale=h_sc[c][:], start=True, stop=True,
+                rhs=h_codes[c][:, i0:i1].bitcast(FP8X4), rhs_scale=h_sc[c][:, i0:i1], start=True, stop=True,
             )
 
         neg_logits = keep.tile([P, I], F32, name="neg_logits", tag=f"h_bf{CHUNKS - 2}", align_bytes=64)

@@ -25,7 +25,7 @@ RUN = 4
 CHUNK = 128
 CHUNKS = I // CHUNK
 Z_BANKS = 7
-WK_FIRST = 896
+WK_FIRST = 1024
 WK_VECTOR_COLS = 72
 LAST_SCALAR_SLOTS = 44
 POOL_SLOTS = 20
@@ -43,7 +43,7 @@ def tile_attend_additiveattn_kernel(tc, enc_words, enc_scales, wk, qterm, gain, 
 
         offsets = keep.tile([P, I // 16], U16, name="offsets")
         pool_scales = keep.tile([P, T], U8, name="pool_scales", tag=AFTER_SCALE_GATHER, align_bytes=BURST)
-        nc.vector.memset(pool_scales[:].bitcast(I32), 0)
+        nc.gpsimd.memset(pool_scales[:].bitcast(I32), 0)
 
         wk_raw = keep.tile([P, PACK, F], F32, name="wk_raw", align_bytes=BURST)
         wk_rows = wk.rearrange("(p j) f -> p (j f)", j=PACK)

@@ -27,8 +27,8 @@ CHUNKS = I // CHUNK
 Z_BANKS = 7
 WK_FIRST = 1024
 WK_VECTOR_COLS = 72
-LAST_SCALAR_SLOTS = 44
-POOL_SLOTS = 20
+LAST_SCALAR_SLOTS = 36
+POOL_SLOTS = 28
 AFTER_WK_QUANTISER = "shared0"
 AFTER_SCALE_GATHER = "shared1"
 
@@ -148,9 +148,9 @@ def tile_attend_additiveattn_kernel(tc, enc_words, enc_scales, wk, qterm, gain, 
                     nc.scalar.activation(h_bf[c][:, w:, t], th[c][:, t, w:], ACT.Copy, scale=gain_cols[:, t : t + 1])
             v = w - POOL_SLOTS
             nc.gpsimd.tensor_tensor(
-                h_bf[c][:, v:w],
-                th[c][:, :, v:w].rearrange("p t i -> p i t"),
-                gain_cols.rearrange("p (i t) -> p i t", i=1).to_broadcast([P, POOL_SLOTS, PACK]),
+                h_bf[c][:, v:w].rearrange("p (a b) t -> p a t b", b=RUN),
+                th[c][:, :, v:w].rearrange("p t (a b) -> p a t b", b=RUN),
+                gain_cols.rearrange("p (a t b) -> p a t b", a=1, b=1).to_broadcast([P, POOL_SLOTS // RUN, PACK, RUN]),
                 ALU.mult,
             )
             w = v

@@ -24,12 +24,13 @@ BURST = 256
 RUN = 4
 CHUNK = 128
 CHUNKS = I // CHUNK
+HALF = CHUNK // 2
 Z_BANKS = 7
 WK_FIRST = 1024
 WK_VECTOR_COLS = 72
-LAST_SCALAR_SLOTS = 36
+LAST_SCALAR_SLOTS = 32
 POOL_SLOTS = 28
-AFTER_WK_QUANTISER = "shared0"
+LAST_POOL_SLOTS = 24
 AFTER_SCALE_GATHER = "shared1"
 
 
@@ -88,8 +89,8 @@ def tile_attend_additiveattn_kernel(tc, enc_words, enc_scales, wk, qterm, gain, 
         nc.sync.dma_start(gain_cols, gain.rearrange("(p t) o -> p (t o)", t=PACK))
 
         wk_bf = [
-            keep.tile([P, 2, P, PACK], BF16, name=f"wk_bf{u}", tag=tag, align_bytes=64)
-            for u, tag in enumerate(("wk_bf0", AFTER_WK_QUANTISER))
+            keep.tile([P, 2, P, PACK], BF16, name=f"wk_bf{u}", align_bytes=64)
+            for u in range(2)
         ]
         src = wk_raw[:].rearrange("p j (m t) -> p m j t", t=PACK)
         dst = [wk_bf[u][:].rearrange("p e m j -> p m j e") for u in range(2)]
@@ -104,7 +105,7 @@ def tile_attend_additiveattn_kernel(tc, enc_words, enc_scales, wk, qterm, gain, 
                 wk_codes[u][:].bitcast(FP8X4), wk_sc[u][:], wk_bf[u][:].rearrange("p e m j -> p (e m j)")
             )
 
-        enc_codes = keep.tile([P, I], U32, name="enc_codes", tag=AFTER_WK_QUANTISER, align_bytes=64)
+        enc_codes = keep.tile([P, I], U32, name="enc_codes", align_bytes=64)
         for i0, i1 in ((0, CHUNK), (CHUNK, I // 2), (I // 2, I)):
             nc.vector.tensor_copy(enc_codes[:, i0:i1], pool_words[:].bitcast(U32).indirect(offsets[:, i0 // 16 : i1 // 16]))
 
@@ -127,6 +128,7 @@ def tile_attend_additiveattn_kernel(tc, enc_words, enc_scales, wk, qterm, gain, 
         h_codes = [keep.tile([P, CHUNK], U32, name=f"h_codes{c}", align_bytes=64) for c in range(CHUNKS)]
         h_sc = [keep.tile([P, CHUNK], U8, name=f"h_sc{c}", align_bytes=64) for c in range(CHUNKS)]
         half = I // 2
+        last_z = []
 
         for c in range(CHUNKS):
             i0 = c * CHUNK
@@ -138,28 +140,43 @@ def tile_attend_additiveattn_kernel(tc, enc_words, enc_scales, wk, qterm, gain, 
                     z[:], lhsT=wk_codes[t // 2][:, cols].bitcast(FP8X4), lhsT_scale=wk_sc[t // 2][:, cols],
                     rhs=states.bitcast(FP8X4), rhs_scale=enc_sc[:, i0 : i0 + CHUNK], start=True, stop=True,
                 )
-                nc.scalar.activation(th[c][:, t, :], z[:], ACT.Tanh, bias=q_cols[:, t : t + 1])
+                if c < CHUNKS - 1 or t < PACK // 2:
+                    nc.scalar.activation(th[c][:, t, :], z[:], ACT.Tanh, bias=q_cols[:, t : t + 1])
+                else:
+                    last_z.append((t, z))
+        for i0, i1 in ((0, HALF), (HALF, CHUNK)):
+            for t, z in last_z:
+                nc.scalar.activation(th[CHUNKS - 1][:, t, i0:i1], z[:, i0:i1], ACT.Tanh, bias=q_cols[:, t : t + 1])
+
+        def gain_on_vector(c, i0, i1):
+            nc.vector.tensor_tensor(
+                h_bf[c][:, i0:i1].rearrange("p (a b) t -> p a t b", b=RUN),
+                th[c][:, :, i0:i1].rearrange("p t (a b) -> p a t b", b=RUN),
+                gain_bank[:, :, 0:1].rearrange("p (a t) b -> p a t b", a=1).to_broadcast([P, (i1 - i0) // RUN, PACK, RUN]),
+                ALU.mult,
+            )
+
+        def gain_on_gpsimd(c, i0, i1):
+            nc.gpsimd.tensor_tensor(
+                h_bf[c][:, i0:i1].rearrange("p (a b) t -> p a t b", b=RUN),
+                th[c][:, :, i0:i1].rearrange("p t (a b) -> p a t b", b=RUN),
+                gain_cols.rearrange("p (a t b) -> p a t b", a=1, b=1).to_broadcast([P, (i1 - i0) // RUN, PACK, RUN]),
+                ALU.mult,
+            )
+
+        def gain_on_scalar(c, i0, i1):
+            for t in range(PACK):
+                nc.scalar.activation(h_bf[c][:, i0:i1, t], th[c][:, t, i0:i1], ACT.Copy, scale=gain_cols[:, t : t + 1])
 
         def apply_gain(c):
-            w = CHUNK
-            if c == CHUNKS - 1:
-                w = CHUNK - LAST_SCALAR_SLOTS
-                for t in range(PACK):
-                    nc.scalar.activation(h_bf[c][:, w:, t], th[c][:, t, w:], ACT.Copy, scale=gain_cols[:, t : t + 1])
-            v = w - POOL_SLOTS
-            nc.gpsimd.tensor_tensor(
-                h_bf[c][:, v:w].rearrange("p (a b) t -> p a t b", b=RUN),
-                th[c][:, :, v:w].rearrange("p t (a b) -> p a t b", b=RUN),
-                gain_cols.rearrange("p (a t b) -> p a t b", a=1, b=1).to_broadcast([P, POOL_SLOTS // RUN, PACK, RUN]),
-                ALU.mult,
-            )
-            w = v
-            nc.vector.tensor_tensor(
-                h_bf[c][:, :w].rearrange("p (a b) t -> p a t b", b=RUN),
-                th[c][:, :, :w].rearrange("p t (a b) -> p a t b", b=RUN),
-                gain_bank[:, :, 0:1].rearrange("p (a t) b -> p a t b", a=1).to_broadcast([P, w // RUN, PACK, RUN]),
-                ALU.mult,
-            )
+            if c < CHUNKS - 1:
+                gain_on_gpsimd(c, CHUNK - POOL_SLOTS, CHUNK)
+                gain_on_vector(c, 0, CHUNK - POOL_SLOTS)
+            else:
+                gain_on_gpsimd(c, HALF - LAST_POOL_SLOTS, HALF)
+                gain_on_vector(c, 0, HALF - LAST_POOL_SLOTS)
+                gain_on_scalar(c, CHUNK - LAST_SCALAR_SLOTS, CHUNK)
+                gain_on_vector(c, HALF, CHUNK - LAST_SCALAR_SLOTS)
 
         def quantize_h(c, i0, i1):
             nc.vector.quantize_mx(

from contextlib import ExitStack

import concourse.mybir as mybir
from concourse.masks import make_identity

K, T, I, F, M = 512, 2048, 512, 512, 128
FLOPS = 2 * K * F * I + 2 * F * M * I

F32 = mybir.dt.float32
BF16 = mybir.dt.bfloat16
I32 = mybir.dt.int32
U32 = mybir.dt.uint32
U16 = mybir.dt.uint16
U8 = mybir.dt.uint8
FP8X4 = mybir.dt.float8_e4m3fn_x4
ACT = mybir.ActivationFunctionType
ALU = mybir.AluOpType

P = 128
PACK = 4
QUADRANT = 32
ROW_FIRST, ROW_STEP = 32, 4
BURST = 256
RUN = 4
CHUNK = 128
CHUNKS = I // CHUNK
HALF = CHUNK // 2
Z_BANKS = 7
WK_FIRST = 1024
WK_VECTOR_COLS = 72
LAST_SCALAR_SLOTS = 32
POOL_SLOTS = 28
LAST_POOL_SLOTS = 24
AFTER_SCALE_GATHER = "shared1"


def tile_attend_additiveattn_kernel(tc, enc_words, enc_scales, wk, qterm, gain, score, offs, out):
    nc = tc.nc
    with ExitStack() as ctx:
        keep = ctx.enter_context(tc.tile_pool(name="keep", bufs=1))
        zpool = ctx.enter_context(tc.psum_pool(name="zpool", bufs=Z_BANKS))

        gpool = ctx.enter_context(tc.psum_pool(name="gpool", bufs=1))

        offsets = keep.tile([P, I // 16], U16, name="offsets")
        pool_scales = keep.tile([P, T], U8, name="pool_scales", tag=AFTER_SCALE_GATHER, align_bytes=BURST)
        nc.gpsimd.memset(pool_scales[:].bitcast(I32), 0)

        wk_raw = keep.tile([P, PACK, F], F32, name="wk_raw", align_bytes=BURST)
        wk_rows = wk.rearrange("(p j) f -> p (j f)", j=PACK)
        wk_flat = wk_raw[:].rearrange("p j f -> p (j f)")
        nc.sync.dma_start(wk_flat[:, :WK_FIRST], wk_rows[:, :WK_FIRST])
        nc.sync.dma_start(offsets[:], offs)
        nc.sync.dma_start(pool_scales[ROW_FIRST : ROW_FIRST + 16 * ROW_STEP : ROW_STEP, :].bitcast(I32), enc_scales[0].bitcast(I32))
        nc.sync.dma_start(wk_flat[:, WK_FIRST:], wk_rows[:, WK_FIRST:])

        enc_sc = keep.tile([P, I], U8, name="enc_sc", align_bytes=BURST)
        nc.gpsimd.memset(enc_sc[:].bitcast(I32), 0)
        gain_row = keep.tile([P, F + RUN], F32, name="gain_row", align_bytes=BURST)
        nc.gpsimd.memset(gain_row[:], 0.0)
        warm_out = keep.tile([P, 1], F32, name="warm_out")
        nc.scalar.activation(warm_out[:], gain_row[:, F : F + 1], ACT.Exp)

        nc.sync.dma_start(gain_row[0:1, :F], gain.rearrange("f o -> o f"))
        identity = keep.tile([P, P], F32, name="identity")
        make_identity(nc, identity[:])
        gain_bank = gpool.tile([P, PACK, P], F32, name="gain_bank")
        for t in range(PACK):
            nc.tensor.transpose(gain_bank[:, t, :], gain_row[:, t:F:PACK], identity[:])

        pool_words = keep.tile([P, T], I32, name="pool_words", align_bytes=BURST)
        nc.sync.dma_start(pool_words[:], enc_words[0].rearrange("p n r -> p (n r)").bitcast(I32))

        picked_sc = keep.tile([P, I], U8, name="picked_sc", align_bytes=BURST)
        nc.vector.tensor_copy(picked_sc[:], pool_scales[:].indirect(offsets[:]))
        for r in range(4):
            first = ROW_FIRST + ROW_STEP * r
            nc.sync.dma_start(
                enc_sc[r:P:QUADRANT, :].bitcast(I32),
                picked_sc[first : first + 16 * ROW_STEP : 4 * ROW_STEP, :].bitcast(I32),
            )

        late = keep.tile([P, PACK * M + 4 * PACK], F32, name="late", tag=AFTER_SCALE_GATHER, align_bytes=BURST)
        score_raw = late[:, : PACK * M]
        q_cols = late[:, PACK * M : PACK * M + PACK]
        gain_cols = late[:, PACK * M + 2 * PACK : PACK * M + 3 * PACK]
        nc.sync.dma_start(q_cols, qterm.rearrange("(p t) o -> p (t o)", t=PACK))
        nc.sync.dma_start(score_raw, score.rearrange("(p j) m -> p (j m)", j=PACK))
        nc.sync.dma_start(gain_cols, gain.rearrange("(p t) o -> p (t o)", t=PACK))

        wk_bf = [
            keep.tile([P, 2, P, PACK], BF16, name=f"wk_bf{u}", align_bytes=64)
            for u in range(2)
        ]
        src = wk_raw[:].rearrange("p j (m t) -> p m j t", t=PACK)
        dst = [wk_bf[u][:].rearrange("p e m j -> p m j e") for u in range(2)]
        for u in range(2):
            pair = src[:, :, :, 2 * u : 2 * u + 2]
            nc.vector.tensor_copy(dst[u][:, :WK_VECTOR_COLS], pair[:, :WK_VECTOR_COLS])
            nc.scalar.activation(dst[u][:, WK_VECTOR_COLS:], pair[:, WK_VECTOR_COLS:], ACT.Copy)
        wk_codes = [keep.tile([P, 2 * P], U32, name=f"wk_codes{u}", align_bytes=64) for u in range(2)]
        wk_sc = [keep.tile([P, 2 * P], U8, name=f"wk_sc{u}", align_bytes=64) for u in range(2)]
        for u in range(2):
            nc.vector.quantize_mx(
                wk_codes[u][:].bitcast(FP8X4), wk_sc[u][:], wk_bf[u][:].rearrange("p e m j -> p (e m j)")
            )

        enc_codes = keep.tile([P, I], U32, name="enc_codes", align_bytes=64)
        for i0, i1 in ((0, CHUNK), (CHUNK, I // 2), (I // 2, I)):
            nc.vector.tensor_copy(enc_codes[:, i0:i1], pool_words[:].bitcast(U32).indirect(offsets[:, i0 // 16 : i1 // 16]))

        score_bf = [keep.tile([P, M // 2, PACK], BF16, name=f"score_bf{h}", align_bytes=64) for h in range(2)]
        score_codes = keep.tile([P, M], U32, name="score_codes", align_bytes=64)
        score_sc = keep.tile([P, M], U8, name="score_sc", align_bytes=64)
        for h in range(2):
            nc.vector.tensor_copy(
                score_bf[h][:].rearrange("p (a b) j -> p a j b", b=RUN),
                score_raw.rearrange("p (j a b) -> p a j b", j=PACK, b=RUN)[:, h * M // (2 * RUN) : (h + 1) * M // (2 * RUN)],
            )
        for h in range(2):
            heads = slice(h * M // 2, (h + 1) * M // 2)
            nc.vector.quantize_mx(
                score_codes[:, heads].bitcast(FP8X4), score_sc[:, heads], score_bf[h][:].rearrange("p m j -> p (m j)")
            )

        th = [keep.tile([P, PACK, CHUNK], F32, name=f"th{c}") for c in range(CHUNKS)]
        h_bf = [keep.tile([P, CHUNK, PACK], BF16, name=f"h_bf{c}", tag=f"h_bf{c}", align_bytes=64) for c in range(CHUNKS)]
        h_codes = [keep.tile([P, CHUNK], U32, name=f"h_codes{c}", align_bytes=64) for c in range(CHUNKS)]
        h_sc = [keep.tile([P, CHUNK], U8, name=f"h_sc{c}", align_bytes=64) for c in range(CHUNKS)]
        half = I // 2
        last_z = []

        for c in range(CHUNKS):
            i0 = c * CHUNK
            states = enc_codes[:, i0 : i0 + CHUNK]
            for t in range(PACK):
                cols = slice(t % 2 * P, (t % 2 + 1) * P)
                z = zpool.tile([P, CHUNK], F32, name="z")
                nc.tensor.matmul_mx(
                    z[:], lhsT=wk_codes[t // 2][:, cols].bitcast(FP8X4), lhsT_scale=wk_sc[t // 2][:, cols],
                    rhs=states.bitcast(FP8X4), rhs_scale=enc_sc[:, i0 : i0 + CHUNK], start=True, stop=True,
                )
                if c < CHUNKS - 1 or t < PACK // 2:
                    nc.scalar.activation(th[c][:, t, :], z[:], ACT.Tanh, bias=q_cols[:, t : t + 1])
                else:
                    last_z.append((t, z))
        for i0, i1 in ((0, HALF), (HALF, CHUNK)):
            for t, z in last_z:
                nc.scalar.activation(th[CHUNKS - 1][:, t, i0:i1], z[:, i0:i1], ACT.Tanh, bias=q_cols[:, t : t + 1])

        def gain_on_vector(c, i0, i1):
            nc.vector.tensor_tensor(
                h_bf[c][:, i0:i1].rearrange("p (a b) t -> p a t b", b=RUN),
                th[c][:, :, i0:i1].rearrange("p t (a b) -> p a t b", b=RUN),
                gain_bank[:, :, 0:1].rearrange("p (a t) b -> p a t b", a=1).to_broadcast([P, (i1 - i0) // RUN, PACK, RUN]),
                ALU.mult,
            )

        def gain_on_gpsimd(c, i0, i1):
            nc.gpsimd.tensor_tensor(
                h_bf[c][:, i0:i1].rearrange("p (a b) t -> p a t b", b=RUN),
                th[c][:, :, i0:i1].rearrange("p t (a b) -> p a t b", b=RUN),
                gain_cols.rearrange("p (a t b) -> p a t b", a=1, b=1).to_broadcast([P, (i1 - i0) // RUN, PACK, RUN]),
                ALU.mult,
            )

        def gain_on_scalar(c, i0, i1):
            for t in range(PACK):
                nc.scalar.activation(h_bf[c][:, i0:i1, t], th[c][:, t, i0:i1], ACT.Copy, scale=gain_cols[:, t : t + 1])

        def apply_gain(c):
            if c < CHUNKS - 1:
                gain_on_gpsimd(c, CHUNK - POOL_SLOTS, CHUNK)
                gain_on_vector(c, 0, CHUNK - POOL_SLOTS)
            else:
                gain_on_gpsimd(c, HALF - LAST_POOL_SLOTS, HALF)
                gain_on_vector(c, 0, HALF - LAST_POOL_SLOTS)
                gain_on_scalar(c, CHUNK - LAST_SCALAR_SLOTS, CHUNK)
                gain_on_vector(c, HALF, CHUNK - LAST_SCALAR_SLOTS)

        def quantize_h(c, i0, i1):
            nc.vector.quantize_mx(
                h_codes[c][:, i0:i1].bitcast(FP8X4), h_sc[c][:, i0:i1], h_bf[c][:, i0:i1].rearrange("p i t -> p (i t)")
            )

        logits_a = zpool.tile([P, half], F32, name="logits_a", tag="z")
        logits_b = zpool.tile([P, half], F32, name="logits_b", tag="z")

        apply_gain(0)
        for c in range(1, CHUNKS):
            apply_gain(c)
            quantize_h(c - 1, 0, CHUNK)
        pieces = [(c, 0, CHUNK) for c in range(CHUNKS - 1)] + [(CHUNKS - 1, 0, CHUNK // 2), (CHUNKS - 1, CHUNK // 2, CHUNK)]
        for c, i0, i1 in pieces[CHUNKS - 1 :]:
            quantize_h(c, i0, i1)
        for c, i0, i1 in pieces:
            nc.tensor.matmul_mx(
                (logits_a, logits_b)[c // 2][:, c % 2 * CHUNK + i0 : c % 2 * CHUNK + i1],
                lhsT=score_codes[:].bitcast(FP8X4), lhsT_scale=score_sc[:],
                rhs=h_codes[c][:, i0:i1].bitcast(FP8X4), rhs_scale=h_sc[c][:, i0:i1], start=True, stop=True,
            )

        neg_logits = keep.tile([P, I], F32, name="neg_logits", tag=f"h_bf{CHUNKS - 2}", align_bytes=64)
        neg_max_a = keep.tile([P, 1], F32, name="neg_max_a")
        nc.vector.tensor_scalar(neg_logits[:, :half], logits_a[:], -1.0, None, ALU.mult, ALU.min, accum_out=neg_max_a[:])
        neg_max = keep.tile([P, 1], F32, name="neg_max")
        nc.vector.tensor_scalar(neg_logits[:, half:], logits_b[:], -1.0, neg_max_a[:], ALU.mult, ALU.min, accum_out=neg_max[:])

        p_exp = keep.tile([P, I], F32, name="p_exp")
        row_sum = keep.tile([P, 1], F32, name="row_sum")
        nc.scalar.activation(p_exp[:], neg_logits[:], ACT.Exp, bias=neg_max[:], scale=-1.0, accum_out=row_sum[:])
        inv_sum = keep.tile([P, 1], F32, name="inv_sum")
        nc.vector.reciprocal(inv_sum[:], row_sum[:])
        result = keep.tile([P, I], F32, name="result", align_bytes=BURST)
        nc.vector.tensor_scalar(result[:], p_exp[:], inv_sum[:], 512.0, ALU.mult, ALU.mult)
        nc.sync.dma_start(out, result[:])
